import numpy as np
import ml_dtypes


def mxq(x, axis, fmt="e4m3"):
    dtype, down = {"e4m3": (ml_dtypes.float8_e4m3fn, 7), "e5m2": (ml_dtypes.float8_e5m2, 14)}[fmt]
    v = np.moveaxis(np.asarray(x, np.float32).astype(ml_dtypes.bfloat16).astype(np.float64), axis, -1)
    blocks = v.reshape(v.shape[:-1] + (-1, 32))
    amax = np.abs(blocks).max(-1, keepdims=True)
    byte = np.maximum(np.where(amax > 0, np.frexp(amax)[1] - 1 + 127, 0) - down, 1)
    scale = np.exp2(byte - 127.0)
    codes = (blocks / scale).astype(np.float32).astype(dtype).astype(np.float64)
    return np.moveaxis((codes * scale).reshape(v.shape), -1, axis)


WIDE = False


def mx_kscale(k):
    if not WIDE:
        return np.ones(k)
    levels = np.array([10, -10, 5, -5, 0])
    if k % 512:
        return np.exp2(np.random.permutation(np.resize(levels, k // 32))).repeat(32)
    a = np.empty((k // 512, 16))
    for p in range(k // 512):
        a[p, :8] = np.random.permutation(np.resize(levels, 8))
        for g in range(8):
            far = levels[np.abs(levels - a[p, g]) >= 10]
            a[p, g + 8] = far[np.random.randint(len(far))]
    return np.exp2(a.ravel()).repeat(32)


def f64(x):
    return np.asarray(x).astype(np.float64)


def striped(idx):
    return np.tile(idx.reshape(-1, 16).T, (8, 1)).astype(np.uint16)


def unstriped(offs):
    return offs[:16].T.reshape(-1).astype(np.int64)


K, T, S, N = 1024, 2048, 512, 256


def setup_inputs():
    n = np.random.standard_normal
    s = mx_kscale(K)[:, None]
    return {
        "xT": (n((K, T)) * s).astype(np.float32),
        "w1": (n((K, N)) / np.sqrt(K) / s).astype(np.float32),
        "w2": (n((K, N)) / np.sqrt(K) / s).astype(np.float32),
        "w3": (n((K, N)) / np.sqrt(K) / s).astype(np.float32),
        "offs": striped(np.random.permutation(T)[:S]),
    }


def reference(xT, w1, w2, w3, offs):
    xq = mxq(f64(xT)[:, unstriped(offs)], 0, "e4m3")
    return np.minimum(np.minimum(mxq(f64(w1), 0, "e4m3").T @ xq, mxq(f64(w2), 0, "e4m3").T @ xq), mxq(f64(w3), 0, "e4m3").T @ xq)

@@ -1,0 +1,146 @@
+from contextlib import ExitStack
+
+import concourse.mybir as mybir
+
+K, T, S, N = 1024, 2048, 512, 256
+FLOPS = 3 * 2 * K * S * N
+
+F32 = mybir.dt.float32
+BF16 = mybir.dt.bfloat16
+U32 = mybir.dt.uint32
+U16 = mybir.dt.uint16
+U8 = mybir.dt.uint8
+FP8X4 = mybir.dt.float8_e4m3fn_x4
+MIN = mybir.AluOpType.min
+
+P = 128
+PACK = 4
+K_PASS = P * PACK
+PASSES = K // K_PASS
+M_TILES = N // P
+RUN = 4
+
+
+def tile_picked_maxout_min_e_kernel(tc, xT, w1, w2, w3, offs, out):
+    nc = tc.nc
+    weights = (w1, w2, w3)
+    with ExitStack() as ctx:
+        keep = ctx.enter_context(tc.tile_pool(name="keep", bufs=1))
+        psum = ctx.enter_context(tc.psum_pool(name="psum", bufs=1))
+
+        offsets = keep.tile([P, S // 16], U16, name="offsets")
+        planes, w_raw = {}, {}
+
+        def load_plane(g, j):
+            planes[g, j] = keep.tile([P, T], F32, name=f"plane{g}{j}")
+            rows = xT[g * K_PASS : (g + 1) * K_PASS, :].rearrange("(p j) t -> p j t", j=PACK)
+            nc.sync.dma_start(out=planes[g, j][:], in_=rows[:, j, :])
+
+        def load_w(i, g):
+            w_raw[i, g] = keep.tile([P, PACK, N], F32, name=f"w_raw{i}{g}")
+            rows = weights[i][g * K_PASS : (g + 1) * K_PASS, :].rearrange("(p j) n -> p j n", j=PACK)
+            nc.sync.dma_start(out=w_raw[i, g][:], in_=rows)
+
+        load_plane(0, 0)
+        nc.sync.dma_start(offsets[:], offs)
+        for j in range(1, PACK):
+            load_plane(0, j)
+        load_w(0, 0)
+        for j in range(PACK):
+            load_plane(1, j)
+        for i, g in ((0, 1), (1, 0), (1, 1), (2, 0), (2, 1)):
+            load_w(i, g)
+
+        x_codes, x_scales = {}, {}
+
+        def gather_pass(g):
+            picked = keep.tile([P, S, PACK], BF16, name=f"picked{g}", align_bytes=64)
+            for j in range(PACK):
+                nc.vector.tensor_copy(picked[:, :, j], planes[g, j][:].indirect(offsets[:]))
+            x_codes[g] = keep.tile([P, S], U32, name=f"x_codes{g}", align_bytes=64)
+            x_scales[g] = keep.tile([P, S], U8, name=f"x_scales{g}", align_bytes=64)
+            nc.vector.quantize_mx(out=x_codes[g][:].bitcast(FP8X4), scales=x_scales[g][:],
+                                  in_=picked[:].rearrange("p s j -> p (s j)"))
+
+        w_bf, w_codes, w_scales = {}, {}, {}
+
+        def weave(i, g, m0, m1, engine):
+            width = (m1 - m0) * P
+            w_bf[i, g, m0] = keep.tile([P, width, PACK], BF16, name=f"w_bf{i}{g}{m0}", align_bytes=64)
+            dst = w_bf[i, g, m0][:].rearrange("p (c r) j -> p c j r", r=RUN)
+            src = w_raw[i, g][:, :, m0 * P : m1 * P].rearrange("p j (c r) -> p c j r", r=RUN)
+            if engine == "scalar":
+                nc.scalar.copy(dst, src)
+            else:
+                nc.vector.tensor_copy(dst, src)
+
+        def quant(i, g, m0, m1):
+            width = (m1 - m0) * P
+            codes = keep.tile([P, width], U32, name=f"w_codes{i}{g}{m0}", align_bytes=64)
+            scales = keep.tile([P, width], U8, name=f"w_scales{i}{g}{m0}", align_bytes=64)
+            nc.vector.quantize_mx(out=codes[:].bitcast(FP8X4), scales=scales[:],
+                                  in_=w_bf[i, g, m0][:].rearrange("p n j -> p (n j)"))
+            for m in range(m0, m1):
+                cols = slice((m - m0) * P, (m - m0 + 1) * P)
+                w_codes[i, g, m] = codes[:, cols]
+                w_scales[i, g, m] = scales[:, cols]
+
+        acc = {}
+
+        def mm(i, g, m):
+            if g == 0:
+                acc[i, m] = psum.tile([P, S], F32, name=f"acc{i}{m}")
+            nc.tensor.matmul_mx(out=acc[i, m][:], lhsT=w_codes[i, g, m].bitcast(FP8X4), lhsT_scale=w_scales[i, g, m],
+                                rhs=x_codes[g][:].bitcast(FP8X4), rhs_scale=x_scales[g][:],
+                                start=(g == 0), stop=(g == PASSES - 1))
+
+        first, second, result = {}, {}, {}
+
+        def evac(m):
+            first[m] = keep.tile([P, S], F32, name=f"first{m}")
+            nc.scalar.copy(first[m][:], acc[0, m][:])
+
+        def min2(m):
+            second[m] = keep.tile([P, S], F32, name=f"second{m}")
+            nc.vector.tensor_tensor(second[m][:], acc[1, m][:], first[m][:], MIN)
+
+        def min3(m):
+            result[m] = keep.tile([P, S], F32, name=f"result{m}")
+            nc.vector.tensor_tensor(result[m][:], acc[2, m][:], second[m][:], MIN)
+            queue = nc.sync if m == 0 else nc.scalar
+            queue.dma_start(out=out[m * P : (m + 1) * P, :], in_=result[m][:])
+
+        gather_pass(0)
+        weave(0, 0, 0, 2, "scalar")
+        quant(0, 0, 0, 2)
+        mm(0, 0, 0)
+        mm(0, 0, 1)
+        gather_pass(1)
+        weave(0, 1, 0, 2, "scalar")
+        quant(0, 1, 0, 2)
+        mm(0, 1, 0)
+        mm(0, 1, 1)
+        weave(1, 0, 0, 2, "scalar")
+        evac(0)
+        evac(1)
+        weave(1, 1, 0, 2, "vector")
+        quant(1, 0, 0, 2)
+        quant(1, 1, 0, 2)
+        mm(1, 0, 0)
+        mm(1, 1, 0)
+        mm(1, 0, 1)
+        mm(1, 1, 1)
+        weave(2, 0, 0, 2, "scalar")
+        min2(0)
+        quant(2, 0, 0, 2)
+        mm(2, 0, 0)
+        mm(2, 0, 1)
+        weave(2, 1, 0, 1, "scalar")
+        weave(2, 1, 1, 2, "scalar")
+        min2(1)
+        quant(2, 1, 0, 1)
+        mm(2, 1, 0)
+        quant(2, 1, 1, 2)
+        mm(2, 1, 1)
+        min3(0)
+        min3(1)

@@ -19,6 +19,7 @@ K_PASS = P * PACK
 PASSES = K // K_PASS
 M_TILES = N // P
 RUN = 4
+H = S // 2
 
 
 def tile_picked_maxout_min_e_kernel(tc, xT, w1, w2, w3, offs, out):
@@ -36,20 +37,22 @@ def tile_picked_maxout_min_e_kernel(tc, xT, w1, w2, w3, offs, out):
             rows = xT[g * K_PASS : (g + 1) * K_PASS, :].rearrange("(p j) t -> p j t", j=PACK)
             nc.sync.dma_start(out=planes[g, j][:], in_=rows[:, j, :])
 
-        def load_w(i, g):
-            w_raw[i, g] = keep.tile([P, PACK, N], F32, name=f"w_raw{i}{g}")
-            rows = weights[i][g * K_PASS : (g + 1) * K_PASS, :].rearrange("(p j) n -> p j n", j=PACK)
-            nc.sync.dma_start(out=w_raw[i, g][:], in_=rows)
+        def load_w(i, g, m0, m1):
+            raw = keep.tile([P, PACK, (m1 - m0) * P], F32, name=f"w_raw{i}{g}{m0}")
+            rows = weights[i][g * K_PASS : (g + 1) * K_PASS, m0 * P : m1 * P].rearrange("(p j) n -> p j n", j=PACK)
+            nc.sync.dma_start(out=raw[:], in_=rows)
+            w_raw[i, g, m0] = raw
 
         load_plane(0, 0)
         nc.sync.dma_start(offsets[:], offs)
         for j in range(1, PACK):
             load_plane(0, j)
-        load_w(0, 0)
         for j in range(PACK):
             load_plane(1, j)
-        for i, g in ((0, 1), (1, 0), (1, 1), (2, 0), (2, 1)):
-            load_w(i, g)
+        for i, g in ((0, 0), (0, 1), (1, 0), (1, 1), (2, 0)):
+            load_w(i, g, 0, 2)
+        load_w(2, 1, 0, 1)
+        load_w(2, 1, 1, 2)
 
         x_codes, x_scales = {}, {}
 
@@ -65,10 +68,10 @@ def tile_picked_maxout_min_e_kernel(tc, xT, w1, w2, w3, offs, out):
         w_bf, w_codes, w_scales = {}, {}, {}
 
         def weave(i, g, m0, m1, engine):
-            width = (m1 - m0) * P
-            w_bf[i, g, m0] = keep.tile([P, width, PACK], BF16, name=f"w_bf{i}{g}{m0}", align_bytes=64)
-            dst = w_bf[i, g, m0][:].rearrange("p (c r) j -> p c j r", r=RUN)
-            src = w_raw[i, g][:, :, m0 * P : m1 * P].rearrange("p j (c r) -> p c j r", r=RUN)
+            if m0 == 0:
+                w_bf[i, g] = keep.tile([P, N, PACK], BF16, name=f"w_bf{i}{g}", tag="w_bf", bufs=2, align_bytes=64)
+            dst = w_bf[i, g][:, m0 * P : m1 * P, :].rearrange("p (c r) j -> p c j r", r=RUN)
+            src = w_raw[i, g, m0][:].rearrange("p j (c r) -> p c j r", r=RUN)
             if engine == "scalar":
                 nc.scalar.copy(dst, src)
             else:
@@ -79,7 +82,7 @@ def tile_picked_maxout_min_e_kernel(tc, xT, w1, w2, w3, offs, out):
             codes = keep.tile([P, width], U32, name=f"w_codes{i}{g}{m0}", align_bytes=64)
             scales = keep.tile([P, width], U8, name=f"w_scales{i}{g}{m0}", align_bytes=64)
             nc.vector.quantize_mx(out=codes[:].bitcast(FP8X4), scales=scales[:],
-                                  in_=w_bf[i, g, m0][:].rearrange("p n j -> p (n j)"))
+                                  in_=w_bf[i, g][:, m0 * P : m1 * P, :].rearrange("p n j -> p (n j)"))
             for m in range(m0, m1):
                 cols = slice((m - m0) * P, (m - m0 + 1) * P)
                 w_codes[i, g, m] = codes[:, cols]
@@ -87,39 +90,38 @@ def tile_picked_maxout_min_e_kernel(tc, xT, w1, w2, w3, offs, out):
 
         acc = {}
 
-        def mm(i, g, m):
+        def mm(i, g, m, c0=0, c1=S):
             if g == 0:
-                acc[i, m] = psum.tile([P, S], F32, name=f"acc{i}{m}")
-            nc.tensor.matmul_mx(out=acc[i, m][:], lhsT=w_codes[i, g, m].bitcast(FP8X4), lhsT_scale=w_scales[i, g, m],
-                                rhs=x_codes[g][:].bitcast(FP8X4), rhs_scale=x_scales[g][:],
+                acc[i, m, c0] = psum.tile([P, c1 - c0], F32, name=f"acc{i}{m}{c0}")
+            nc.tensor.matmul_mx(out=acc[i, m, c0][:], lhsT=w_codes[i, g, m].bitcast(FP8X4), lhsT_scale=w_scales[i, g, m],
+                                rhs=x_codes[g][:, c0:c1].bitcast(FP8X4), rhs_scale=x_scales[g][:, c0:c1],
                                 start=(g == 0), stop=(g == PASSES - 1))
 
-        first, second, result = {}, {}, {}
+        first, second = {}, {}
 
         def evac(m):
             first[m] = keep.tile([P, S], F32, name=f"first{m}")
-            nc.scalar.copy(first[m][:], acc[0, m][:])
+            nc.scalar.copy(first[m][:], acc[0, m, 0][:])
 
         def min2(m):
             second[m] = keep.tile([P, S], F32, name=f"second{m}")
-            nc.vector.tensor_tensor(second[m][:], acc[1, m][:], first[m][:], MIN)
+            nc.vector.tensor_tensor(second[m][:], acc[1, m, 0][:], first[m][:], MIN)
 
-        def min3(m):
-            result[m] = keep.tile([P, S], F32, name=f"result{m}")
-            nc.vector.tensor_tensor(result[m][:], acc[2, m][:], second[m][:], MIN)
-            queue = nc.sync if m == 0 else nc.scalar
-            queue.dma_start(out=out[m * P : (m + 1) * P, :], in_=result[m][:])
+        def min3(m, h):
+            cols = slice(h * H, (h + 1) * H)
+            third = acc[2, m, 0][:, cols] if m == 0 else acc[2, m, h * H][:]
+            result = keep.tile([P, H], F32, name=f"result{m}{h}")
+            nc.vector.tensor_tensor(result[:], third, second[m][:, cols], MIN)
+            queue = nc.sync if h == 0 else nc.scalar
+            queue.dma_start(out=out[m * P : (m + 1) * P, cols], in_=result[:])
 
         gather_pass(0)
-        weave(0, 0, 0, 2, "scalar")
-        quant(0, 0, 0, 2)
-        mm(0, 0, 0)
-        mm(0, 0, 1)
         gather_pass(1)
-        weave(0, 1, 0, 2, "scalar")
-        quant(0, 1, 0, 2)
-        mm(0, 1, 0)
-        mm(0, 1, 1)
+        for g in range(PASSES):
+            weave(0, g, 0, 2, "scalar")
+            quant(0, g, 0, 2)
+            mm(0, g, 0)
+            mm(0, g, 1)
         weave(1, 0, 0, 2, "scalar")
         evac(0)
         evac(1)
@@ -130,17 +132,20 @@ def tile_picked_maxout_min_e_kernel(tc, xT, w1, w2, w3, offs, out):
         mm(1, 1, 0)
         mm(1, 0, 1)
         mm(1, 1, 1)
-        weave(2, 0, 0, 2, "scalar")
-        min2(0)
+        weave(2, 0, 0, 2, "vector")
         quant(2, 0, 0, 2)
         mm(2, 0, 0)
-        mm(2, 0, 1)
+        mm(2, 0, 1, 0, H)
+        mm(2, 0, 1, H, S)
+        min2(0)
         weave(2, 1, 0, 1, "scalar")
         weave(2, 1, 1, 2, "scalar")
-        min2(1)
         quant(2, 1, 0, 1)
         mm(2, 1, 0)
+        min2(1)
         quant(2, 1, 1, 2)
-        mm(2, 1, 1)
-        min3(0)
-        min3(1)
+        mm(2, 1, 1, 0, H)
+        mm(2, 1, 1, H, S)
+        for m in range(M_TILES):
+            for h in range(2):
+                min3(m, h)

@@ -32,120 +32,175 @@ def tile_picked_maxout_min_e_kernel(tc, xT, w1, w2, w3, offs, out):
         offsets = keep.tile([P, S // 16], U16, name="offsets")
         planes, w_raw = {}, {}
 
-        def load_plane(g, j):
-            planes[g, j] = keep.tile([P, T], F32, name=f"plane{g}{j}")
-            rows = xT[g * K_PASS : (g + 1) * K_PASS, :].rearrange("(p j) t -> p j t", j=PACK)
-            nc.sync.dma_start(out=planes[g, j][:], in_=rows[:, j, :])
+        def load_planes(g, j0, j1):
+            tile = keep.tile([P, (j1 - j0) * T], F32, name=f"plane{g}{j0}", tag=f"plane{g}{j0}", align_bytes=64)
+            rows = xT[g * K_PASS : (g + 1) * K_PASS, :].rearrange("(p j) t -> p (j t)", j=PACK)
+            nc.sync.dma_start(out=tile[:], in_=rows[:, j0 * T : j1 * T])
+            for j in range(j0, j1):
+                planes[g, j] = tile[:, (j - j0) * T : (j - j0 + 1) * T]
 
         def load_w(i, g, m0, m1):
-            raw = keep.tile([P, PACK, (m1 - m0) * P], F32, name=f"w_raw{i}{g}{m0}")
+            raw = keep.tile([P, PACK, (m1 - m0) * P], F32, name=f"w_raw{i}{g}{m0}", tag=f"w_raw{i}{g}{m0}", align_bytes=64)
             rows = weights[i][g * K_PASS : (g + 1) * K_PASS, m0 * P : m1 * P].rearrange("(p j) n -> p j n", j=PACK)
             nc.sync.dma_start(out=raw[:], in_=rows)
-            w_raw[i, g, m0] = raw
+            for m in range(m0, m1):
+                w_raw[i, g, m] = (raw, (m - m0) * P)
 
-        load_plane(0, 0)
-        nc.sync.dma_start(offsets[:], offs)
-        for j in range(1, PACK):
-            load_plane(0, j)
-        for j in range(PACK):
-            load_plane(1, j)
-        for i, g in ((0, 0), (0, 1), (1, 0), (1, 1), (2, 0)):
-            load_w(i, g, 0, 2)
-        load_w(2, 1, 0, 1)
-        load_w(2, 1, 1, 2)
+        picked, x_codes, x_scales = {}, {}, {}
 
-        x_codes, x_scales = {}, {}
+        def gather(g, j, c0=0, c1=S):
+            if g not in picked:
+                picked[g] = keep.tile([P, S, PACK], BF16, name=f"picked{g}", tag=f"picked{g}", align_bytes=64)
+            nc.vector.tensor_copy(picked[g][:, c0:c1, j], planes[g, j].indirect(offsets[:, c0 // 16 : c1 // 16]))
 
-        def gather_pass(g):
-            picked = keep.tile([P, S, PACK], BF16, name=f"picked{g}", align_bytes=64)
-            for j in range(PACK):
-                nc.vector.tensor_copy(picked[:, :, j], planes[g, j][:].indirect(offsets[:]))
-            x_codes[g] = keep.tile([P, S], U32, name=f"x_codes{g}", align_bytes=64)
-            x_scales[g] = keep.tile([P, S], U8, name=f"x_scales{g}", align_bytes=64)
-            nc.vector.quantize_mx(out=x_codes[g][:].bitcast(FP8X4), scales=x_scales[g][:],
-                                  in_=picked[:].rearrange("p s j -> p (s j)"))
+        def quant_x(g, c0=0, c1=S):
+            if g not in x_codes:
+                x_codes[g] = keep.tile([P, S], U32, name=f"x_codes{g}", align_bytes=64)
+                x_scales[g] = keep.tile([P, S], U8, name=f"x_scales{g}", align_bytes=64)
+            nc.vector.quantize_mx(out=x_codes[g][:, c0:c1].bitcast(FP8X4), scales=x_scales[g][:, c0:c1],
+                                  in_=picked[g][:, c0:c1, :].rearrange("p s j -> p (s j)"))
 
         w_bf, w_codes, w_scales = {}, {}, {}
 
-        def weave(i, g, m0, m1, engine):
-            if m0 == 0:
-                w_bf[i, g] = keep.tile([P, N, PACK], BF16, name=f"w_bf{i}{g}", tag="w_bf", bufs=2, align_bytes=64)
-            dst = w_bf[i, g][:, m0 * P : m1 * P, :].rearrange("p (c r) j -> p c j r", r=RUN)
-            src = w_raw[i, g, m0][:].rearrange("p j (c r) -> p c j r", r=RUN)
+        def new_bf(i, g, m0, m1, tag=None, bufs=1):
+            tile = keep.tile([P, (m1 - m0) * P, PACK], BF16, name=f"w_bf{i}{g}{m0}", tag=tag or f"w_bf{i}{g}{m0}", bufs=bufs, align_bytes=64)
+            for m in range(m0, m1):
+                w_bf[i, g, m] = (tile, (m - m0) * P)
+
+        def weave(i, g, m, engine, c0=0, c1=P, tag=None, bufs=1):
+            if (i, g, m) not in w_bf:
+                new_bf(i, g, m, m + (c1 + P - 1) // P, tag, bufs)
+            tile, at = w_bf[i, g, m]
+            raw, raw_at = w_raw[i, g, m]
+            dst = tile[:, at + c0 : at + c1, :].rearrange("p (c r) j -> p c j r", r=RUN)
+            src = raw[:, :, raw_at + c0 : raw_at + c1].rearrange("p j (c r) -> p c j r", r=RUN)
             if engine == "scalar":
                 nc.scalar.copy(dst, src)
+            elif engine == "gpsimd":
+                nc.gpsimd.tensor_copy(dst, src)
             else:
                 nc.vector.tensor_copy(dst, src)
 
-        def quant(i, g, m0, m1):
+        def quant(i, g, m0, m1=None, tag=None):
+            m1 = m1 or m0 + 1
             width = (m1 - m0) * P
-            codes = keep.tile([P, width], U32, name=f"w_codes{i}{g}{m0}", align_bytes=64)
-            scales = keep.tile([P, width], U8, name=f"w_scales{i}{g}{m0}", align_bytes=64)
+            codes = keep.tile([P, width], U32, name=f"w_codes{i}{g}{m0}", tag=tag or f"w_codes{i}{g}{m0}", align_bytes=64)
+            scales = keep.tile([P, width], U8, name=f"w_scales{i}{g}{m0}", tag=f"w_scales{i}{g}{m0}", align_bytes=64)
+            tile, at = w_bf[i, g, m0]
             nc.vector.quantize_mx(out=codes[:].bitcast(FP8X4), scales=scales[:],
-                                  in_=w_bf[i, g][:, m0 * P : m1 * P, :].rearrange("p n j -> p (n j)"))
+                                  in_=tile[:, at : at + width, :].rearrange("p n j -> p (n j)"))
             for m in range(m0, m1):
                 cols = slice((m - m0) * P, (m - m0 + 1) * P)
                 w_codes[i, g, m] = codes[:, cols]
                 w_scales[i, g, m] = scales[:, cols]
 
-        acc = {}
+        acc, passes_done = {}, {}
 
-        def mm(i, g, m, c0=0, c1=S):
-            if g == 0:
-                acc[i, m, c0] = psum.tile([P, c1 - c0], F32, name=f"acc{i}{m}{c0}")
+        def mm(i, g, m, c0=0, c1=S, tag=None):
+            done = passes_done.get((i, m, c0), 0)
+            passes_done[i, m, c0] = done + 1
+            if done == 0:
+                acc[i, m, c0] = psum.tile([P, c1 - c0], F32, name=f"acc{i}{m}{c0}", tag=tag or f"acc{i}{m}{c0}")
             nc.tensor.matmul_mx(out=acc[i, m, c0][:], lhsT=w_codes[i, g, m].bitcast(FP8X4), lhsT_scale=w_scales[i, g, m],
                                 rhs=x_codes[g][:, c0:c1].bitcast(FP8X4), rhs_scale=x_scales[g][:, c0:c1],
-                                start=(g == 0), stop=(g == PASSES - 1))
+                                start=(done == 0), stop=(done == PASSES - 1))
+
+        def bank(i, m, c0, c1):
+            if (i, m, c0) in acc:
+                return acc[i, m, c0][:, 0 : c1 - c0]
+            return acc[i, m, 0][:, c0:c1]
 
         first, second = {}, {}
 
-        def evac(m):
-            first[m] = keep.tile([P, S], F32, name=f"first{m}")
-            nc.scalar.copy(first[m][:], acc[0, m, 0][:])
+        def evac(m, c0=0, c1=S, i=0):
+            if m not in first:
+                first[m] = keep.tile([P, S], F32, name=f"first{m}", tag=f"first{m}", align_bytes=64)
+            nc.scalar.copy(first[m][:, c0:c1], bank(i, m, c0, c1))
 
-        def min2(m):
-            second[m] = keep.tile([P, S], F32, name=f"second{m}")
-            nc.vector.tensor_tensor(second[m][:], acc[1, m, 0][:], first[m][:], MIN)
+        def min2(m, c0=0, c1=S, i=1, tag=None):
+            if m not in second:
+                second[m] = keep.tile([P, S], F32, name=f"second{m}", tag=tag or f"second{m}", align_bytes=64)
+            nc.vector.tensor_tensor(second[m][:, c0:c1], bank(i, m, c0, c1), first[m][:, c0:c1], MIN)
 
-        def min3(m, h):
-            cols = slice(h * H, (h + 1) * H)
-            third = acc[2, m, 0][:, cols] if m == 0 else acc[2, m, h * H][:]
-            result = keep.tile([P, H], F32, name=f"result{m}{h}")
-            nc.vector.tensor_tensor(result[:], third, second[m][:, cols], MIN)
-            queue = nc.sync if h == 0 else nc.scalar
-            queue.dma_start(out=out[m * P : (m + 1) * P, cols], in_=result[:])
+        def min3(m, c0, c1, queue, i=2):
+            result = keep.tile([P, c1 - c0], F32, name=f"result{m}{c0}")
+            nc.vector.tensor_tensor(result[:], bank(i, m, c0, c1), second[m][:, c0:c1], MIN)
+            queue.dma_start(out=out[m * P : (m + 1) * P, c0:c1], in_=result[:])
 
-        gather_pass(0)
-        gather_pass(1)
-        for g in range(PASSES):
-            weave(0, g, 0, 2, "scalar")
-            quant(0, g, 0, 2)
-            mm(0, g, 0)
-            mm(0, g, 1)
-        weave(1, 0, 0, 2, "scalar")
-        evac(0)
+        def clock(ap):
+            probe = keep.tile([P, 1], ap.dtype, name="probe", tag="probe", bufs=8)
+            nc.gpsimd.tensor_copy(probe[:], ap)
+
+        load_planes(0, 0, 1)
+        nc.sync.dma_start(offsets[:], offs)
+        for j in range(1, PACK):
+            load_planes(0, j, j + 1)
+        for j in range(PACK - 1):
+            load_planes(1, j, j + 1)
+        load_w(0, 0, 0, 2)
+        load_planes(1, 3, 4)
+        for i, g in ((0, 1), (1, 0), (1, 1), (2, 0)):
+            load_w(i, g, 0, 2)
+        load_w(2, 1, 0, 1)
+        load_w(2, 1, 1, 2)
+        for j in range(PACK):
+            gather(0, j)
+        quant_x(0)
+        for j in range(PACK - 1):
+            gather(1, j)
+        weave(0, 0, 0, "vector", tag="plane12")
+        weave(0, 0, 1, "vector", tag="plane11")
+        quant(0, 0, 0)
+        quant(0, 0, 1)
+        mm(0, 0, 0, 0, H)
+        mm(0, 0, 0, H, S)
+        mm(0, 0, 1)
+        gather(1, 3, 0, H)
+        gather(1, 3, H, S)
+        quant_x(1, 0, H)
+        quant_x(1, H, S)
+        weave(0, 1, 0, "scalar")
+        weave(0, 1, 1, "scalar")
+        quant(0, 1, 0)
+        quant(0, 1, 1)
+        mm(0, 1, 0, 0, H)
+        mm(0, 1, 0, H, S)
+        mm(0, 1, 1)
+        weave(1, 0, 0, "vector", tag="w_raw010")
+        weave(1, 0, 1, "scalar")
+        quant(1, 0, 0)
+        quant(1, 0, 1)
+        evac(0, 0, H)
+        evac(0, H, S)
         evac(1)
-        weave(1, 1, 0, 2, "vector")
-        quant(1, 0, 0, 2)
-        quant(1, 1, 0, 2)
-        mm(1, 0, 0)
-        mm(1, 1, 0)
+        weave(1, 1, 0, "vector", tag="w_raw100")
+        weave(1, 1, 1, "vector", tag="w_bf101")
+        quant(1, 1, 0)
+        quant(1, 1, 1)
+        mm(1, 0, 0, 0, H)
+        mm(1, 0, 0, H, S)
+        mm(1, 1, 0, 0, H)
+        mm(1, 1, 0, H, S)
         mm(1, 0, 1)
         mm(1, 1, 1)
-        weave(2, 0, 0, 2, "vector")
-        quant(2, 0, 0, 2)
+        weave(2, 0, 0, "vector", tag="w_raw100")
+        weave(2, 0, 1, "scalar", tag="w_codes011")
+        min2(0, 0, H)
+        quant(2, 0, 0)
+        min2(0, H, S)
+        weave(2, 1, 0, "scalar", tag="w_scales011")
+        quant(2, 0, 1)
+        quant(2, 1, 0)
         mm(2, 0, 0)
-        mm(2, 0, 1, 0, H)
-        mm(2, 0, 1, H, S)
-        min2(0)
-        weave(2, 1, 0, 1, "scalar")
-        weave(2, 1, 1, 2, "scalar")
-        quant(2, 1, 0, 1)
+        mm(2, 0, 1, 0, H, tag="acc000")
+        mm(2, 0, 1, H, S, tag="acc00256")
         mm(2, 1, 0)
-        min2(1)
-        quant(2, 1, 1, 2)
+        min2(1, tag="w_raw210")
+        weave(2, 1, 1, "scalar", tag="w_codes110")
+        quant(2, 1, 1)
         mm(2, 1, 1, 0, H)
         mm(2, 1, 1, H, S)
-        for m in range(M_TILES):
-            for h in range(2):
-                min3(m, h)
+        min3(0, 0, H, nc.sync)
+        min3(0, H, S, nc.scalar)
+        min3(1, 0, H, nc.sync)
+        min3(1, H, S, nc.scalar)

@@ -48,9 +48,9 @@ def tile_picked_maxout_min_e_kernel(tc, xT, w1, w2, w3, offs, out):
 
         picked, x_codes, x_scales = {}, {}, {}
 
-        def gather(g, j, c0=0, c1=S):
+        def gather(g, j, c0=0, c1=S, tag=None):
             if g not in picked:
-                picked[g] = keep.tile([P, S, PACK], BF16, name=f"picked{g}", tag=f"picked{g}", align_bytes=64)
+                picked[g] = keep.tile([P, S, PACK], BF16, name=f"picked{g}", tag=tag or f"picked{g}", align_bytes=64)
             nc.vector.tensor_copy(picked[g][:, c0:c1, j], planes[g, j].indirect(offsets[:, c0 // 16 : c1 // 16]))
 
         def quant_x(g, c0=0, c1=S):
@@ -113,18 +113,16 @@ def tile_picked_maxout_min_e_kernel(tc, xT, w1, w2, w3, offs, out):
         first, second = {}, {}
 
         def evac(m, c0=0, c1=S, i=0):
-            if m not in first:
-                first[m] = keep.tile([P, S], F32, name=f"first{m}", tag=f"first{m}", align_bytes=64)
-            nc.scalar.copy(first[m][:, c0:c1], bank(i, m, c0, c1))
+            first[m, c0] = keep.tile([P, c1 - c0], F32, name=f"first{m}{c0}", tag=f"first{m}{c0}", align_bytes=64)
+            nc.scalar.copy(first[m, c0][:], bank(i, m, c0, c1))
 
         def min2(m, c0=0, c1=S, i=1, tag=None):
-            if m not in second:
-                second[m] = keep.tile([P, S], F32, name=f"second{m}", tag=tag or f"second{m}", align_bytes=64)
-            nc.vector.tensor_tensor(second[m][:, c0:c1], bank(i, m, c0, c1), first[m][:, c0:c1], MIN)
+            second[m, c0] = keep.tile([P, c1 - c0], F32, name=f"second{m}{c0}", tag=tag or f"second{m}{c0}", align_bytes=64)
+            nc.vector.tensor_tensor(second[m, c0][:], bank(i, m, c0, c1), first[m, c0][:, 0 : c1 - c0] if (m, c0) in first else first[m, 0][:, c0:c1], MIN)
 
         def min3(m, c0, c1, queue, i=2):
             result = keep.tile([P, c1 - c0], F32, name=f"result{m}{c0}")
-            nc.vector.tensor_tensor(result[:], bank(i, m, c0, c1), second[m][:, c0:c1], MIN)
+            nc.vector.tensor_tensor(result[:], bank(i, m, c0, c1), second[m, c0][:, 0 : c1 - c0] if (m, c0) in second else second[m, 0][:, c0:c1], MIN)
             queue.dma_start(out=out[m * P : (m + 1) * P, c0:c1], in_=result[:])
 
         def clock(ap):
@@ -169,13 +167,13 @@ def tile_picked_maxout_min_e_kernel(tc, xT, w1, w2, w3, offs, out):
         weave(1, 0, 0, "vector", tag="w_raw010")
         weave(1, 0, 1, "scalar")
         quant(1, 0, 0)
-        quant(1, 0, 1)
         evac(0, 0, H)
         evac(0, H, S)
         evac(1)
         weave(1, 1, 0, "vector", tag="w_raw100")
-        weave(1, 1, 1, "vector", tag="w_bf101")
+        weave(1, 1, 1, "vector", tag="w_raw010")
         quant(1, 1, 0)
+        quant(1, 0, 1, tag="w_raw110")
         quant(1, 1, 1)
         mm(1, 0, 0, 0, H)
         mm(1, 0, 0, H, S)
@@ -191,13 +189,16 @@ def tile_picked_maxout_min_e_kernel(tc, xT, w1, w2, w3, offs, out):
         weave(2, 1, 0, "scalar", tag="w_scales011")
         quant(2, 0, 1)
         quant(2, 1, 0)
-        mm(2, 0, 0)
+        mm(2, 0, 0, 0, H)
+        mm(2, 0, 0, H, S)
         mm(2, 0, 1, 0, H, tag="acc000")
         mm(2, 0, 1, H, S, tag="acc00256")
-        mm(2, 1, 0)
-        min2(1, tag="w_raw210")
+        mm(2, 1, 0, 0, H)
+        mm(2, 1, 0, H, S)
+        min2(1, 0, H, tag="w_raw210")
         weave(2, 1, 1, "scalar", tag="w_codes110")
         quant(2, 1, 1)
+        min2(1, H, S, tag="w_raw211")
         mm(2, 1, 1, 0, H)
         mm(2, 1, 1, H, S)
         min3(0, 0, H, nc.sync)

@@ -125,10 +125,6 @@ def tile_picked_maxout_min_e_kernel(tc, xT, w1, w2, w3, offs, out):
             nc.vector.tensor_tensor(result[:], bank(i, m, c0, c1), second[m, c0][:, 0 : c1 - c0] if (m, c0) in second else second[m, 0][:, c0:c1], MIN)
             queue.dma_start(out=out[m * P : (m + 1) * P, c0:c1], in_=result[:])
 
-        def clock(ap):
-            probe = keep.tile([P, 1], ap.dtype, name="probe", tag="probe", bufs=8)
-            nc.gpsimd.tensor_copy(probe[:], ap)
-
         load_planes(0, 0, 1)
         nc.sync.dma_start(offsets[:], offs)
         for j in range(1, PACK):
@@ -195,10 +191,9 @@ def tile_picked_maxout_min_e_kernel(tc, xT, w1, w2, w3, offs, out):
         mm(2, 0, 1, H, S, tag="acc00256")
         mm(2, 1, 0, 0, H)
         mm(2, 1, 0, H, S)
-        min2(1, 0, H, tag="w_raw210")
+        min2(1, 0, S, tag="w_raw210")
         weave(2, 1, 1, "scalar", tag="w_codes110")
         quant(2, 1, 1)
-        min2(1, H, S, tag="w_raw211")
         mm(2, 1, 1, 0, H)
         mm(2, 1, 1, H, S)
         min3(0, 0, H, nc.sync)

@@ -20,6 +20,7 @@ PASSES = K // K_PASS
 M_TILES = N // P
 RUN = 4
 H = S // 2
+ALIGN = 256
 
 
 def tile_picked_maxout_min_e_kernel(tc, xT, w1, w2, w3, offs, out):
@@ -33,14 +34,14 @@ def tile_picked_maxout_min_e_kernel(tc, xT, w1, w2, w3, offs, out):
         planes, w_raw = {}, {}
 
         def load_planes(g, j0, j1):
-            tile = keep.tile([P, (j1 - j0) * T], F32, name=f"plane{g}{j0}", tag=f"plane{g}{j0}", align_bytes=64)
+            tile = keep.tile([P, (j1 - j0) * T], F32, name=f"plane{g}{j0}", tag=f"plane{g}{j0}", align_bytes=ALIGN)
             rows = xT[g * K_PASS : (g + 1) * K_PASS, :].rearrange("(p j) t -> p (j t)", j=PACK)
             nc.sync.dma_start(out=tile[:], in_=rows[:, j0 * T : j1 * T])
             for j in range(j0, j1):
                 planes[g, j] = tile[:, (j - j0) * T : (j - j0 + 1) * T]
 
         def load_w(i, g, m0, m1):
-            raw = keep.tile([P, PACK, (m1 - m0) * P], F32, name=f"w_raw{i}{g}{m0}", tag=f"w_raw{i}{g}{m0}", align_bytes=64)
+            raw = keep.tile([P, PACK, (m1 - m0) * P], F32, name=f"w_raw{i}{g}{m0}", tag=f"w_raw{i}{g}{m0}", align_bytes=ALIGN)
             rows = weights[i][g * K_PASS : (g + 1) * K_PASS, m0 * P : m1 * P].rearrange("(p j) n -> p j n", j=PACK)
             nc.sync.dma_start(out=raw[:], in_=rows)
             for m in range(m0, m1):
@@ -50,20 +51,20 @@ def tile_picked_maxout_min_e_kernel(tc, xT, w1, w2, w3, offs, out):
 
         def gather(g, j, c0=0, c1=S, tag=None):
             if g not in picked:
-                picked[g] = keep.tile([P, S, PACK], BF16, name=f"picked{g}", tag=tag or f"picked{g}", align_bytes=64)
+                picked[g] = keep.tile([P, S, PACK], BF16, name=f"picked{g}", tag=tag or f"picked{g}", align_bytes=ALIGN)
             nc.vector.tensor_copy(picked[g][:, c0:c1, j], planes[g, j].indirect(offsets[:, c0 // 16 : c1 // 16]))
 
         def quant_x(g, c0=0, c1=S):
             if g not in x_codes:
-                x_codes[g] = keep.tile([P, S], U32, name=f"x_codes{g}", align_bytes=64)
-                x_scales[g] = keep.tile([P, S], U8, name=f"x_scales{g}", align_bytes=64)
+                x_codes[g] = keep.tile([P, S], U32, name=f"x_codes{g}", align_bytes=ALIGN)
+                x_scales[g] = keep.tile([P, S], U8, name=f"x_scales{g}", align_bytes=ALIGN)
             nc.vector.quantize_mx(out=x_codes[g][:, c0:c1].bitcast(FP8X4), scales=x_scales[g][:, c0:c1],
                                   in_=picked[g][:, c0:c1, :].rearrange("p s j -> p (s j)"))
 
         w_bf, w_codes, w_scales = {}, {}, {}
 
         def new_bf(i, g, m0, m1, tag=None, bufs=1):
-            tile = keep.tile([P, (m1 - m0) * P, PACK], BF16, name=f"w_bf{i}{g}{m0}", tag=tag or f"w_bf{i}{g}{m0}", bufs=bufs, align_bytes=64)
+            tile = keep.tile([P, (m1 - m0) * P, PACK], BF16, name=f"w_bf{i}{g}{m0}", tag=tag or f"w_bf{i}{g}{m0}", bufs=bufs, align_bytes=ALIGN)
             for m in range(m0, m1):
                 w_bf[i, g, m] = (tile, (m - m0) * P)
 
@@ -84,8 +85,8 @@ def tile_picked_maxout_min_e_kernel(tc, xT, w1, w2, w3, offs, out):
         def quant(i, g, m0, m1=None, tag=None):
             m1 = m1 or m0 + 1
             width = (m1 - m0) * P
-            codes = keep.tile([P, width], U32, name=f"w_codes{i}{g}{m0}", tag=tag or f"w_codes{i}{g}{m0}", align_bytes=64)
-            scales = keep.tile([P, width], U8, name=f"w_scales{i}{g}{m0}", tag=f"w_scales{i}{g}{m0}", align_bytes=64)
+            codes = keep.tile([P, width], U32, name=f"w_codes{i}{g}{m0}", tag=tag or f"w_codes{i}{g}{m0}", align_bytes=ALIGN)
+            scales = keep.tile([P, width], U8, name=f"w_scales{i}{g}{m0}", tag=f"w_scales{i}{g}{m0}", align_bytes=ALIGN)
             tile, at = w_bf[i, g, m0]
             nc.vector.quantize_mx(out=codes[:].bitcast(FP8X4), scales=scales[:],
                                   in_=tile[:, at : at + width, :].rearrange("p n j -> p (n j)"))
@@ -113,15 +114,15 @@ def tile_picked_maxout_min_e_kernel(tc, xT, w1, w2, w3, offs, out):
         first, second = {}, {}
 
         def evac(m, c0=0, c1=S, i=0):
-            first[m, c0] = keep.tile([P, c1 - c0], F32, name=f"first{m}{c0}", tag=f"first{m}{c0}", align_bytes=64)
+            first[m, c0] = keep.tile([P, c1 - c0], F32, name=f"first{m}{c0}", tag=f"first{m}{c0}", align_bytes=ALIGN)
             nc.scalar.copy(first[m, c0][:], bank(i, m, c0, c1))
 
         def min2(m, c0=0, c1=S, i=1, tag=None):
-            second[m, c0] = keep.tile([P, c1 - c0], F32, name=f"second{m}{c0}", tag=tag or f"second{m}{c0}", align_bytes=64)
+            second[m, c0] = keep.tile([P, c1 - c0], F32, name=f"second{m}{c0}", tag=tag or f"second{m}{c0}", align_bytes=ALIGN)
             nc.vector.tensor_tensor(second[m, c0][:], bank(i, m, c0, c1), first[m, c0][:, 0 : c1 - c0] if (m, c0) in first else first[m, 0][:, c0:c1], MIN)
 
         def min3(m, c0, c1, queue, i=2):
-            result = keep.tile([P, c1 - c0], F32, name=f"result{m}{c0}")
+            result = keep.tile([P, c1 - c0], F32, name=f"result{m}{c0}", align_bytes=ALIGN)
             nc.vector.tensor_tensor(result[:], bank(i, m, c0, c1), second[m, c0][:, 0 : c1 - c0] if (m, c0) in second else second[m, 0][:, c0:c1], MIN)
             queue.dma_start(out=out[m * P : (m + 1) * P, c0:c1], in_=result[:])
 

@@ -106,6 +106,11 @@ def tile_picked_maxout_min_e_kernel(tc, xT, w1, w2, w3, offs, out):
                                 rhs=x_codes[g][:, c0:c1].bitcast(FP8X4), rhs_scale=x_scales[g][:, c0:c1],
                                 start=(done == 0), stop=(done == PASSES - 1))
 
+        def warm_up(tag):
+            unread = psum.tile([P, S], F32, name="unread", tag=tag)
+            nc.tensor.matmul_mx(out=unread[:], lhsT=w_codes[0, 0, 1].bitcast(FP8X4), lhsT_scale=w_scales[0, 0, 1],
+                                rhs=x_codes[0][:].bitcast(FP8X4), rhs_scale=x_scales[0][:], start=True, stop=True)
+
         def bank(i, m, c0, c1):
             if (i, m, c0) in acc:
                 return acc[i, m, c0][:, 0 : c1 - c0]
@@ -150,6 +155,8 @@ def tile_picked_maxout_min_e_kernel(tc, xT, w1, w2, w3, offs, out):
         mm(0, 0, 0, 0, H)
         mm(0, 0, 0, H, S)
         mm(0, 0, 1)
+        warm_up("acc200")
+        warm_up("acc20256")
         gather(1, 3, 0, H)
         gather(1, 3, H, S)
         quant_x(1, 0, H)

@@ -12,12 +12,12 @@ U16 = mybir.dt.uint16
 U8 = mybir.dt.uint8
 FP8X4 = mybir.dt.float8_e4m3fn_x4
 MIN = mybir.AluOpType.min
+COPY = mybir.ActivationFunctionType.Copy
 
 P = 128
 PACK = 4
 K_PASS = P * PACK
 PASSES = K // K_PASS
-M_TILES = N // P
 RUN = 4
 H = S // 2
 ALIGN = 256
@@ -30,51 +30,10 @@ def tile_picked_maxout_min_e_kernel(tc, xT, w1, w2, w3, offs, out):
         keep = ctx.enter_context(tc.tile_pool(name="keep", bufs=1))
         psum = ctx.enter_context(tc.psum_pool(name="psum", bufs=1))
 
-        offsets = keep.tile([P, S // 16], U16, name="offsets")
-        planes, w_raw = {}, {}
+        def sbuf(shape, dtype, name, tag=None):
+            return keep.tile(shape, dtype, name=name, tag=tag or name, align_bytes=ALIGN)
 
-        def load_planes(g, j0, j1):
-            tile = keep.tile([P, (j1 - j0) * T], F32, name=f"plane{g}{j0}", tag=f"plane{g}{j0}", align_bytes=ALIGN)
-            rows = xT[g * K_PASS : (g + 1) * K_PASS, :].rearrange("(p j) t -> p (j t)", j=PACK)
-            nc.sync.dma_start(out=tile[:], in_=rows[:, j0 * T : j1 * T])
-            for j in range(j0, j1):
-                planes[g, j] = tile[:, (j - j0) * T : (j - j0 + 1) * T]
-
-        def load_w(i, g, m0, m1):
-            raw = keep.tile([P, PACK, (m1 - m0) * P], F32, name=f"w_raw{i}{g}{m0}", tag=f"w_raw{i}{g}{m0}", align_bytes=ALIGN)
-            rows = weights[i][g * K_PASS : (g + 1) * K_PASS, m0 * P : m1 * P].rearrange("(p j) n -> p j n", j=PACK)
-            nc.sync.dma_start(out=raw[:], in_=rows)
-            for m in range(m0, m1):
-                w_raw[i, g, m] = (raw, (m - m0) * P)
-
-        picked, x_codes, x_scales = {}, {}, {}
-
-        def gather(g, j, c0=0, c1=S, tag=None):
-            if g not in picked:
-                picked[g] = keep.tile([P, S, PACK], BF16, name=f"picked{g}", tag=tag or f"picked{g}", align_bytes=ALIGN)
-            nc.vector.tensor_copy(picked[g][:, c0:c1, j], planes[g, j].indirect(offsets[:, c0 // 16 : c1 // 16]))
-
-        def quant_x(g, c0=0, c1=S):
-            if g not in x_codes:
-                x_codes[g] = keep.tile([P, S], U32, name=f"x_codes{g}", align_bytes=ALIGN)
-                x_scales[g] = keep.tile([P, S], U8, name=f"x_scales{g}", align_bytes=ALIGN)
-            nc.vector.quantize_mx(out=x_codes[g][:, c0:c1].bitcast(FP8X4), scales=x_scales[g][:, c0:c1],
-                                  in_=picked[g][:, c0:c1, :].rearrange("p s j -> p (s j)"))
-
-        w_bf, w_codes, w_scales = {}, {}, {}
-
-        def new_bf(i, g, m0, m1, tag=None, bufs=1):
-            tile = keep.tile([P, (m1 - m0) * P, PACK], BF16, name=f"w_bf{i}{g}{m0}", tag=tag or f"w_bf{i}{g}{m0}", bufs=bufs, align_bytes=ALIGN)
-            for m in range(m0, m1):
-                w_bf[i, g, m] = (tile, (m - m0) * P)
-
-        def weave(i, g, m, engine, c0=0, c1=P, tag=None, bufs=1):
-            if (i, g, m) not in w_bf:
-                new_bf(i, g, m, m + (c1 + P - 1) // P, tag, bufs)
-            tile, at = w_bf[i, g, m]
-            raw, raw_at = w_raw[i, g, m]
-            dst = tile[:, at + c0 : at + c1, :].rearrange("p (c r) j -> p c j r", r=RUN)
-            src = raw[:, :, raw_at + c0 : raw_at + c1].rearrange("p j (c r) -> p c j r", r=RUN)
+        def copy(engine, dst, src):
             if engine == "scalar":
                 nc.scalar.copy(dst, src)
             elif engine == "gpsimd":
@@ -82,18 +41,84 @@ def tile_picked_maxout_min_e_kernel(tc, xT, w1, w2, w3, offs, out):
             else:
                 nc.vector.tensor_copy(dst, src)
 
-        def quant(i, g, m0, m1=None, tag=None):
-            m1 = m1 or m0 + 1
-            width = (m1 - m0) * P
-            codes = keep.tile([P, width], U32, name=f"w_codes{i}{g}{m0}", tag=tag or f"w_codes{i}{g}{m0}", align_bytes=ALIGN)
-            scales = keep.tile([P, width], U8, name=f"w_scales{i}{g}{m0}", tag=f"w_scales{i}{g}{m0}", align_bytes=ALIGN)
-            tile, at = w_bf[i, g, m0]
-            nc.vector.quantize_mx(out=codes[:].bitcast(FP8X4), scales=scales[:],
-                                  in_=tile[:, at : at + width, :].rearrange("p n j -> p (n j)"))
+        offsets = keep.tile([P, S // 16], U16, name="offsets")
+        planes, w_raw = {}, {}
+
+        def load_planes(g, j0, j1):
+            tile = sbuf([P, (j1 - j0) * T], F32, f"plane{g}{j0}")
+            rows = xT[g * K_PASS : (g + 1) * K_PASS, :].rearrange("(p j) t -> p (j t)", j=PACK)
+            nc.sync.dma_start(out=tile[:], in_=rows[:, j0 * T : j1 * T])
+            for j in range(j0, j1):
+                planes[g, j] = tile[:, (j - j0) * T : (j - j0 + 1) * T]
+
+        def load_w(i, g, m0, m1, depth=PACK):
+            raw = sbuf([P, depth, (m1 - m0) * P], F32, f"w_raw{i}{g}{m0}")
+            rows = weights[i][g * K_PASS : (g + 1) * K_PASS, m0 * P : m1 * P].rearrange("(p j) n -> p j n", j=PACK)
+            nc.sync.dma_start(out=raw[:, 0:PACK, :], in_=rows)
             for m in range(m0, m1):
-                cols = slice((m - m0) * P, (m - m0 + 1) * P)
-                w_codes[i, g, m] = codes[:, cols]
-                w_scales[i, g, m] = scales[:, cols]
+                w_raw[i, g, m] = (raw, (m - m0) * P)
+
+        picked, flat, x_codes, x_scales = {}, {}, {}, {}
+
+        def window(g, j, c0, c1):
+            return planes[g, j].indirect(offsets[:, c0 // 16 : c1 // 16])
+
+        def picked_tile(g, tag=None):
+            if g not in picked:
+                picked[g] = sbuf([P, S, PACK], BF16, f"picked{g}", tag)
+            return picked[g]
+
+        def gather_step(g, j, c0=0, c1=S, tag=None):
+            nc.vector.tensor_copy(picked_tile(g, tag)[:, c0:c1, j], window(g, j, c0, c1))
+
+        def new_flat(key, count, width, dtype, tag=None):
+            flat[key] = sbuf([P, count, width], dtype, f"flat{key}", tag)
+
+        def gather_flat(engine, key, slot, g, j, c0=0, c1=S, at=0):
+            dst = flat[key][:, slot, at : at + c1 - c0]
+            if engine == "scalar":
+                nc.scalar.activation(dst, window(g, j, c0, c1), COPY)
+            else:
+                nc.vector.tensor_copy(dst, window(g, j, c0, c1))
+
+        def weave_x(engine, key, g, j0, j1, c0=0, c1=S, run=RUN, tag=None):
+            dst = picked_tile(g, tag)[:, c0:c1, j0:j1].rearrange("p (c r) j -> p c j r", r=run)
+            copy(engine, dst, flat[key][:].rearrange("p j (c r) -> p c j r", r=run))
+
+        def place_x(engine, key, g, j, c0, c1):
+            copy(engine, picked_tile(g)[:, c0:c1, j], flat[key][:, 0, :])
+
+        def quant_x(g, c0=0, c1=S, tag=None):
+            if g not in x_codes:
+                x_codes[g] = sbuf([P, S], U32, f"x_codes{g}", tag)
+                x_scales[g] = sbuf([P, S], U8, f"x_scales{g}")
+            nc.vector.quantize_mx(out=x_codes[g][:, c0:c1].bitcast(FP8X4), scales=x_scales[g][:, c0:c1],
+                                  in_=picked[g][:, c0:c1, :].rearrange("p s j -> p (s j)"))
+
+        w_bf, group_tile, w_codes, w_scales = {}, {}, {}, {}
+
+        def group(*members, tag=None):
+            tile = sbuf([P, len(members) * P, PACK], BF16, "w_bf" + "".join(str(v) for v in members[0]), tag)
+            group_tile[members] = tile
+            for at, member in enumerate(members):
+                w_bf[member] = tile[:, at * P : (at + 1) * P, :]
+
+        def weave(i, g, m, engine, c0=0, c1=P, tag=None):
+            if (i, g, m) not in w_bf:
+                group((i, g, m), tag=tag)
+            raw, at = w_raw[i, g, m]
+            dst = w_bf[i, g, m][:, c0:c1, :].rearrange("p (c r) j -> p c j r", r=RUN)
+            copy(engine, dst, raw[:, 0:PACK, at + c0 : at + c1].rearrange("p j (c r) -> p c j r", r=RUN))
+
+        def quant(*members, tag=None, scale_tag=None):
+            name = "".join(str(v) for v in members[0])
+            codes = sbuf([P, len(members) * P], U32, "w_codes" + name, tag)
+            scales = sbuf([P, len(members) * P], U8, "w_scales" + name, scale_tag)
+            nc.vector.quantize_mx(out=codes[:].bitcast(FP8X4), scales=scales[:],
+                                  in_=group_tile[members][:].rearrange("p n j -> p (n j)"))
+            for at, member in enumerate(members):
+                w_codes[member] = codes[:, at * P : (at + 1) * P]
+                w_scales[member] = scales[:, at * P : (at + 1) * P]
 
         acc, passes_done = {}, {}
 
@@ -106,105 +131,136 @@ def tile_picked_maxout_min_e_kernel(tc, xT, w1, w2, w3, offs, out):
                                 rhs=x_codes[g][:, c0:c1].bitcast(FP8X4), rhs_scale=x_scales[g][:, c0:c1],
                                 start=(done == 0), stop=(done == PASSES - 1))
 
-        def warm_up(tag):
-            unread = psum.tile([P, S], F32, name="unread", tag=tag)
-            nc.tensor.matmul_mx(out=unread[:], lhsT=w_codes[0, 0, 1].bitcast(FP8X4), lhsT_scale=w_scales[0, 0, 1],
-                                rhs=x_codes[0][:].bitcast(FP8X4), rhs_scale=x_scales[0][:], start=True, stop=True)
-
         def bank(i, m, c0, c1):
-            if (i, m, c0) in acc:
-                return acc[i, m, c0][:, 0 : c1 - c0]
-            return acc[i, m, 0][:, c0:c1]
+            start = max(k[2] for k in acc if k[:2] == (i, m) and k[2] <= c0)
+            return acc[i, m, start][:, c0 - start : c1 - start]
+
+        def rows_like(flat_ap, shaped):
+            if len(shaped.shape) == 2:
+                return flat_ap
+            return flat_ap.rearrange("p (a b) -> p a b", b=shaped.shape[2])
+
+        def piece(tiles, m, c0, c1):
+            start = max(k[1] for k in tiles if k[0] == m and k[1] <= c0)
+            whole = tiles[m, start]
+            if len(whole.shape) == 2:
+                return whole[:, c0 - start : c1 - start]
+            width = whole.shape[2]
+            return whole[:, (c0 - start) // width : (c1 - start) // width, :]
 
         first, second = {}, {}
 
-        def evac(m, c0=0, c1=S, i=0):
-            first[m, c0] = keep.tile([P, c1 - c0], F32, name=f"first{m}{c0}", tag=f"first{m}{c0}", align_bytes=ALIGN)
-            nc.scalar.copy(first[m, c0][:], bank(i, m, c0, c1))
+        def evac(m, c0=0, c1=S, i=0, tag=None, into=None):
+            first[m, c0] = into if into is not None else sbuf([P, c1 - c0], F32, f"first{m}{c0}", tag)[:]
+            nc.scalar.copy(first[m, c0], rows_like(bank(i, m, c0, c1), first[m, c0]))
 
-        def min2(m, c0=0, c1=S, i=1, tag=None):
-            second[m, c0] = keep.tile([P, c1 - c0], F32, name=f"second{m}{c0}", tag=tag or f"second{m}{c0}", align_bytes=ALIGN)
-            nc.vector.tensor_tensor(second[m, c0][:], bank(i, m, c0, c1), first[m, c0][:, 0 : c1 - c0] if (m, c0) in first else first[m, 0][:, c0:c1], MIN)
+        def minimum(dst, i, m, c0, c1, other):
+            width = min(dst.shape[-1], other.shape[-1])
+            views = []
+            for v in (dst, bank(i, m, c0, c1), other):
+                if len(v.shape) == 2 and width < v.shape[1]:
+                    v = v.rearrange("p (a b) -> p a b", b=width)
+                elif len(v.shape) == 3 and width < v.shape[2]:
+                    v = v.rearrange("p a (c b) -> p a c b", b=width)
+                views.append(v)
+            if max(len(v.shape) for v in views) == 4:
+                rows = [v.shape[1] for v in views if len(v.shape) == 4][0]
+                views = [v if len(v.shape) == 4 else v.rearrange("p (a c) b -> p a c b", a=rows) for v in views]
+            nc.vector.tensor_tensor(views[0], views[1], views[2], MIN)
 
-        def min3(m, c0, c1, queue, i=2):
-            result = keep.tile([P, c1 - c0], F32, name=f"result{m}{c0}", align_bytes=ALIGN)
-            nc.vector.tensor_tensor(result[:], bank(i, m, c0, c1), second[m, c0][:, 0 : c1 - c0] if (m, c0) in second else second[m, 0][:, c0:c1], MIN)
-            queue.dma_start(out=out[m * P : (m + 1) * P, c0:c1], in_=result[:])
+        def min2(m, c0=0, c1=S, i=1, tag=None, into=None):
+            second[m, c0] = into if into is not None else sbuf([P, c1 - c0], F32, f"second{m}{c0}", tag)[:]
+            minimum(second[m, c0], i, m, c0, c1, piece(first, m, c0, c1))
 
-        load_planes(0, 0, 1)
+        def min3(m, c0, c1, queue, i=2, tag=None, into=None):
+            result = into if into is not None else sbuf([P, c1 - c0], F32, f"result{m}{c0}", tag)[:]
+            minimum(result, i, m, c0, c1, piece(second, m, c0, c1))
+            queue.dma_start(out=out[m * P : (m + 1) * P, c0:c1], in_=result)
+
+        load_planes(0, 0, 4)
         nc.sync.dma_start(offsets[:], offs)
-        for j in range(1, PACK):
-            load_planes(0, j, j + 1)
-        for j in range(PACK - 1):
-            load_planes(1, j, j + 1)
+        load_planes(1, 0, 3)
         load_w(0, 0, 0, 2)
         load_planes(1, 3, 4)
-        for i, g in ((0, 1), (1, 0), (1, 1), (2, 0)):
-            load_w(i, g, 0, 2)
+        load_w(0, 1, 0, 2)
+        load_w(1, 0, 0, 2)
+        load_w(1, 1, 0, 2)
+        load_w(2, 0, 0, 2, depth=8)
         load_w(2, 1, 0, 1)
         load_w(2, 1, 1, 2)
-        for j in range(PACK):
-            gather(0, j)
+        new_flat("a", 4, S, F32)
+        gather_flat("scalar", "a", 3, 0, 3)
+        for j in range(3):
+            gather_flat("vector", "a", j, 0, j)
+        weave_x("vector", "a", 0, 0, 4)
         quant_x(0)
-        for j in range(PACK - 1):
-            gather(1, j)
-        weave(0, 0, 0, "vector", tag="plane12")
-        weave(0, 0, 1, "vector", tag="plane11")
-        quant(0, 0, 0)
-        quant(0, 0, 1)
+        new_flat("b", 3, S, F32)
+        gather_flat("scalar", "b", 0, 1, 0)
+        gather_flat("scalar", "b", 1, 1, 1, 0, H)
+        gather_flat("vector", "b", 2, 1, 2)
+        gather_flat("vector", "b", 1, 1, 1, H, S, at=H)
+        weave_x("vector", "b", 1, 0, 3)
+        group((0, 0, 0), (0, 0, 1))
+        weave(0, 0, 0, "scalar")
+        weave(0, 0, 1, "scalar")
+        quant((0, 0, 0), (0, 0, 1))
         mm(0, 0, 0, 0, H)
         mm(0, 0, 0, H, S)
         mm(0, 0, 1)
-        warm_up("acc200")
-        warm_up("acc20256")
-        gather(1, 3, 0, H)
-        gather(1, 3, H, S)
-        quant_x(1, 0, H)
+        new_flat("c", 1, H, BF16)
+        gather_flat("scalar", "c", 0, 1, 3, H, S)
+        gather_step(1, 3, 0, H)
+        place_x("vector", "c", 1, 3, H, S)
+        quant_x(1, 0, H, tag="plane13")
         quant_x(1, H, S)
+        group((0, 1, 1), (1, 0, 0))
         weave(0, 1, 0, "scalar")
         weave(0, 1, 1, "scalar")
-        quant(0, 1, 0)
-        quant(0, 1, 1)
+        quant((0, 1, 0))
         mm(0, 1, 0, 0, H)
         mm(0, 1, 0, H, S)
+        weave(1, 0, 0, "vector")
+        weave(1, 0, 1, "vector")
+        quant((0, 1, 1), (1, 0, 0))
+        quant((1, 0, 1))
         mm(0, 1, 1)
-        weave(1, 0, 0, "vector", tag="w_raw010")
-        weave(1, 0, 1, "scalar")
-        quant(1, 0, 0)
-        evac(0, 0, H)
-        evac(0, H, S)
-        evac(1)
-        weave(1, 1, 0, "vector", tag="w_raw100")
-        weave(1, 1, 1, "vector", tag="w_raw010")
-        quant(1, 1, 0)
-        quant(1, 0, 1, tag="w_raw110")
-        quant(1, 1, 1)
         mm(1, 0, 0, 0, H)
         mm(1, 0, 0, H, S)
+        mm(1, 0, 1)
+        evac(0, 0, H)
+        evac(0, H, S)
+        group((1, 1, 0), (1, 1, 1))
+        weave(1, 1, 0, "scalar")
+        weave(1, 1, 1, "vector")
+        evac(1, into=w_raw[1, 1, 1][0][:, :, P : 2 * P])
+        quant((1, 1, 0), (1, 1, 1))
         mm(1, 1, 0, 0, H)
         mm(1, 1, 0, H, S)
-        mm(1, 0, 1)
         mm(1, 1, 1)
-        weave(2, 0, 0, "vector", tag="w_raw100")
-        weave(2, 0, 1, "scalar", tag="w_codes011")
-        min2(0, 0, H)
-        quant(2, 0, 0)
-        min2(0, H, S)
-        weave(2, 1, 0, "scalar", tag="w_scales011")
-        quant(2, 0, 1)
-        quant(2, 1, 0)
+        group((2, 0, 0), (2, 0, 1))
+        raw3 = w_raw[2, 0, 0][0]
+        weave(2, 0, 1, "vector")
+        weave(2, 0, 0, "scalar", 0, 64)
+        weave(2, 0, 0, "scalar", 64, P)
+        min2(0, 0, H, into=raw3[:, 0:8:2, 0:64])
+        min2(0, H, S, into=raw3[:, 1:8:2, 0:64])
+        quant((2, 0, 0), (2, 0, 1))
         mm(2, 0, 0, 0, H)
         mm(2, 0, 0, H, S)
         mm(2, 0, 1, 0, H, tag="acc000")
         mm(2, 0, 1, H, S, tag="acc00256")
+        min2(1, 0, H, into=raw3[:, 0:PACK, 64:P])
+        weave(2, 1, 0, "scalar")
+        quant((2, 1, 0))
         mm(2, 1, 0, 0, H)
         mm(2, 1, 0, H, S)
-        min2(1, 0, S, tag="w_raw210")
-        weave(2, 1, 1, "scalar", tag="w_codes110")
-        quant(2, 1, 1)
+        min2(1, H, S, tag="w_raw210")
+        weave(2, 1, 1, "scalar")
+        quant((2, 1, 1))
         mm(2, 1, 1, 0, H)
         mm(2, 1, 1, H, S)
-        min3(0, 0, H, nc.sync)
-        min3(0, H, S, nc.scalar)
+        last = w_raw[2, 1, 1][0][:].rearrange("p j n -> p (j n)")
+        min3(0, 0, H, nc.sync, into=last[:, 0:H])
+        min3(0, H, S, nc.scalar, into=last[:, H:S])
         min3(1, 0, H, nc.sync)
         min3(1, H, S, nc.scalar)

@@ -177,33 +177,34 @@ def tile_picked_maxout_min_e_kernel(tc, xT, w1, w2, w3, offs, out):
             minimum(result, i, m, c0, c1, piece(second, m, c0, c1))
             queue.dma_start(out=out[m * P : (m + 1) * P, c0:c1], in_=result)
 
-        load_planes(0, 0, 4)
+        load_planes(0, 0, 1)
         nc.sync.dma_start(offsets[:], offs)
-        load_planes(1, 0, 3)
+        for j in range(1, PACK):
+            load_planes(0, j, j + 1)
+        for j in range(PACK - 1):
+            load_planes(1, j, j + 1)
         load_w(0, 0, 0, 2)
         load_planes(1, 3, 4)
         load_w(0, 1, 0, 2)
-        load_w(1, 0, 0, 2)
+        load_w(1, 0, 0, 2, depth=8)
         load_w(1, 1, 0, 2)
         load_w(2, 0, 0, 2, depth=8)
         load_w(2, 1, 0, 1)
         load_w(2, 1, 1, 2)
-        new_flat("a", 4, S, F32)
-        gather_flat("scalar", "a", 3, 0, 3)
-        for j in range(3):
-            gather_flat("vector", "a", j, 0, j)
-        weave_x("vector", "a", 0, 0, 4)
-        quant_x(0)
-        new_flat("b", 3, S, F32)
-        gather_flat("scalar", "b", 0, 1, 0)
-        gather_flat("scalar", "b", 1, 1, 1, 0, H)
-        gather_flat("vector", "b", 2, 1, 2)
-        gather_flat("vector", "b", 1, 1, 1, H, S, at=H)
-        weave_x("vector", "b", 1, 0, 3)
+        new_flat("a", 1, H, BF16)
+        gather_flat("scalar", "a", 0, 0, 0, H, S)
+        gather_step(0, 0, 0, H)
+        gather_step(0, 1)
+        place_x("vector", "a", 0, 0, H, S)
+        gather_step(0, 2)
+        gather_step(0, 3)
+        for j in range(PACK - 1):
+            gather_step(1, j)
         group((0, 0, 0), (0, 0, 1))
         weave(0, 0, 0, "scalar")
         weave(0, 0, 1, "scalar")
         quant((0, 0, 0), (0, 0, 1))
+        quant_x(0, tag="w_raw000")
         mm(0, 0, 0, 0, H)
         mm(0, 0, 0, H, S)
         mm(0, 0, 1)
@@ -213,27 +214,28 @@ def tile_picked_maxout_min_e_kernel(tc, xT, w1, w2, w3, offs, out):
         place_x("vector", "c", 1, 3, H, S)
         quant_x(1, 0, H, tag="plane13")
         quant_x(1, H, S)
-        group((0, 1, 1), (1, 0, 0))
         weave(0, 1, 0, "scalar")
         weave(0, 1, 1, "scalar")
         quant((0, 1, 0))
         mm(0, 1, 0, 0, H)
         mm(0, 1, 0, H, S)
+        group((1, 0, 0), (1, 0, 1))
         weave(1, 0, 0, "vector")
-        weave(1, 0, 1, "vector")
-        quant((0, 1, 1), (1, 0, 0))
-        quant((1, 0, 1))
+        weave(1, 0, 1, "scalar")
+        quant((0, 1, 1))
         mm(0, 1, 1)
+        quant((1, 0, 0), (1, 0, 1))
         mm(1, 0, 0, 0, H)
         mm(1, 0, 0, H, S)
         mm(1, 0, 1)
-        evac(0, 0, H)
-        evac(0, H, S)
-        group((1, 1, 0), (1, 1, 1))
-        weave(1, 1, 0, "scalar")
+        raw2 = w_raw[1, 0, 0][0]
+        evac(0, 0, H, into=raw2[:, 0:8:2, 0:64])
+        evac(0, H, S, into=raw2[:, 1:8:2, 0:64])
+        evac(1, into=raw2[:, :, 64:P])
+        weave(1, 1, 0, "vector")
         weave(1, 1, 1, "vector")
-        evac(1, into=w_raw[1, 1, 1][0][:, :, P : 2 * P])
-        quant((1, 1, 0), (1, 1, 1))
+        quant((1, 1, 0))
+        quant((1, 1, 1))
         mm(1, 1, 0, 0, H)
         mm(1, 1, 0, H, S)
         mm(1, 1, 1)

@@ -131,6 +131,11 @@ def tile_picked_maxout_min_e_kernel(tc, xT, w1, w2, w3, offs, out):
                                 rhs=x_codes[g][:, c0:c1].bitcast(FP8X4), rhs_scale=x_scales[g][:, c0:c1],
                                 start=(done == 0), stop=(done == PASSES - 1))
 
+        def warm_up(g, c0, c1, tag):
+            unread = psum.tile([P, c1 - c0], F32, name="unread", tag=tag)
+            nc.tensor.matmul_mx(out=unread[:], lhsT=w_codes[0, 0, 1].bitcast(FP8X4), lhsT_scale=w_scales[0, 0, 1],
+                                rhs=x_codes[g][:, c0:c1].bitcast(FP8X4), rhs_scale=x_scales[g][:, c0:c1], start=True, stop=True)
+
         def bank(i, m, c0, c1):
             start = max(k[2] for k in acc if k[:2] == (i, m) and k[2] <= c0)
             return acc[i, m, start][:, c0 - start : c1 - start]
@@ -214,6 +219,8 @@ def tile_picked_maxout_min_e_kernel(tc, xT, w1, w2, w3, offs, out):
         place_x("vector", "c", 1, 3, H, S)
         quant_x(1, 0, H, tag="plane13")
         quant_x(1, H, S)
+        warm_up(1, 0, H, "acc200")
+        warm_up(1, H, S, "acc20256")
         weave(0, 1, 0, "scalar")
         weave(0, 1, 1, "scalar")
         quant((0, 1, 0))

@@ -182,12 +182,10 @@ def tile_picked_maxout_min_e_kernel(tc, xT, w1, w2, w3, offs, out):
             minimum(result, i, m, c0, c1, piece(second, m, c0, c1))
             queue.dma_start(out=out[m * P : (m + 1) * P, c0:c1], in_=result)
 
-        load_planes(0, 0, 1)
+        load_planes(0, 0, 4)
         nc.sync.dma_start(offsets[:], offs)
-        for j in range(1, PACK):
-            load_planes(0, j, j + 1)
-        for j in range(PACK - 1):
-            load_planes(1, j, j + 1)
+        load_planes(1, 0, 2)
+        load_planes(1, 2, 3)
         load_w(0, 0, 0, 2)
         load_planes(1, 3, 4)
         load_w(0, 1, 0, 2)
@@ -196,20 +194,24 @@ def tile_picked_maxout_min_e_kernel(tc, xT, w1, w2, w3, offs, out):
         load_w(2, 0, 0, 2, depth=8)
         load_w(2, 1, 0, 1)
         load_w(2, 1, 1, 2)
-        new_flat("a", 1, H, BF16)
-        gather_flat("scalar", "a", 0, 0, 0, H, S)
-        gather_step(0, 0, 0, H)
-        gather_step(0, 1)
-        place_x("vector", "a", 0, 0, H, S)
-        gather_step(0, 2)
-        gather_step(0, 3)
-        for j in range(PACK - 1):
-            gather_step(1, j)
+        new_flat("a", 4, S, F32)
+        gather_flat("scalar", "a", 3, 0, 3)
+        for j in range(3):
+            gather_flat("vector", "a", j, 0, j)
+        weave_x("vector", "a", 0, 0, 4)
+        quant_x(0)
+        new_flat("b", 2, S, F32)
+        gather_flat("scalar", "b", 0, 1, 0)
+        gather_flat("scalar", "b", 1, 1, 1, H, S, at=H)
+        gather_flat("vector", "b", 1, 1, 1, 0, H)
+        weave_x("vector", "b", 1, 0, 2, run=2)
+        new_flat("d", 1, S, BF16)
+        gather_flat("scalar", "d", 0, 1, 2)
+        place_x("vector", "d", 1, 2, 0, S)
         group((0, 0, 0), (0, 0, 1))
         weave(0, 0, 0, "scalar")
         weave(0, 0, 1, "scalar")
         quant((0, 0, 0), (0, 0, 1))
-        quant_x(0, tag="w_raw000")
         mm(0, 0, 0, 0, H)
         mm(0, 0, 0, H, S)
         mm(0, 0, 1)

@@ -58,6 +58,13 @@ def tile_picked_maxout_min_e_kernel(tc, xT, w1, w2, w3, offs, out):
             for m in range(m0, m1):
                 w_raw[i, g, m] = (raw, (m - m0) * P)
 
+        def load_w_whole(i):
+            raw = sbuf([P, PASSES, PACK * N], F32, f"w_raw{i}")
+            nc.sync.dma_start(out=raw[:], in_=weights[i].rearrange("(g p j) n -> p g (j n)", g=PASSES, j=PACK))
+            for g in range(PASSES):
+                for m in range(2):
+                    w_raw[i, g, m] = (raw[:, g, :].rearrange("p (j n) -> p j n", j=PACK), m * P)
+
         picked, flat, x_codes, x_scales = {}, {}, {}, {}
 
         def window(g, j, c0, c1):
@@ -272,6 +279,6 @@ def tile_picked_maxout_min_e_kernel(tc, xT, w1, w2, w3, offs, out):
         mm(2, 1, 1, H, S)
         last = w_raw[2, 1, 1][0][:].rearrange("p j n -> p (j n)")
         min3(0, 0, H, nc.sync, into=last[:, 0:H])
-        min3(0, H, S, nc.scalar, into=last[:, H:S])
+        min3(0, H, S, nc.sync, into=last[:, H:S])
         min3(1, 0, H, nc.sync)
-        min3(1, H, S, nc.scalar)
+        min3(1, H, S, nc.sync)

@@ -17,7 +17,6 @@ COPY = mybir.ActivationFunctionType.Copy
 P = 128
 PACK = 4
 K_PASS = P * PACK
-PASSES = K // K_PASS
 RUN = 4
 H = S // 2
 ALIGN = 256
@@ -33,252 +32,208 @@ def tile_picked_maxout_min_e_kernel(tc, xT, w1, w2, w3, offs, out):
         def sbuf(shape, dtype, name, tag=None):
             return keep.tile(shape, dtype, name=name, tag=tag or name, align_bytes=ALIGN)
 
-        def copy(engine, dst, src):
-            if engine == "scalar":
-                nc.scalar.copy(dst, src)
-            elif engine == "gpsimd":
-                nc.gpsimd.tensor_copy(dst, src)
-            else:
-                nc.vector.tensor_copy(dst, src)
-
         offsets = keep.tile([P, S // 16], U16, name="offsets")
-        planes, w_raw = {}, {}
+        planes, raw, rows = {}, {}, {}
 
         def load_planes(g, j0, j1):
             tile = sbuf([P, (j1 - j0) * T], F32, f"plane{g}{j0}")
-            rows = xT[g * K_PASS : (g + 1) * K_PASS, :].rearrange("(p j) t -> p (j t)", j=PACK)
-            nc.sync.dma_start(out=tile[:], in_=rows[:, j0 * T : j1 * T])
+            src = xT[g * K_PASS : (g + 1) * K_PASS, :].rearrange("(p j) t -> p (j t)", j=PACK)
+            nc.sync.dma_start(out=tile[:], in_=src[:, j0 * T : j1 * T])
             for j in range(j0, j1):
                 planes[g, j] = tile[:, (j - j0) * T : (j - j0 + 1) * T]
 
-        def load_w(i, g, m0, m1, depth=PACK):
-            raw = sbuf([P, depth, (m1 - m0) * P], F32, f"w_raw{i}{g}{m0}")
-            rows = weights[i][g * K_PASS : (g + 1) * K_PASS, m0 * P : m1 * P].rearrange("(p j) n -> p j n", j=PACK)
-            nc.sync.dma_start(out=raw[:, 0:PACK, :], in_=rows)
-            for m in range(m0, m1):
-                w_raw[i, g, m] = (raw, (m - m0) * P)
-
-        def load_w_whole(i):
-            raw = sbuf([P, PASSES, PACK * N], F32, f"w_raw{i}")
-            nc.sync.dma_start(out=raw[:], in_=weights[i].rearrange("(g p j) n -> p g (j n)", g=PASSES, j=PACK))
-            for g in range(PASSES):
-                for m in range(2):
-                    w_raw[i, g, m] = (raw[:, g, :].rearrange("p (j n) -> p j n", j=PACK), m * P)
-
-        picked, flat, x_codes, x_scales = {}, {}, {}, {}
+        def load_w(i, g, before=0, after=0):
+            tile = sbuf([P, before + PACK + after, N], F32, f"w_raw{i}{g}")
+            src = weights[i][g * K_PASS : (g + 1) * K_PASS, :].rearrange("(p j) n -> p j n", j=PACK)
+            nc.sync.dma_start(out=tile[:, before : before + PACK, :], in_=src)
+            raw[i, g] = tile
+            rows[i, g] = tile[:, before : before + PACK, :]
 
         def window(g, j, c0, c1):
             return planes[g, j].indirect(offsets[:, c0 // 16 : c1 // 16])
 
-        def picked_tile(g, tag=None):
-            if g not in picked:
-                picked[g] = sbuf([P, S, PACK], BF16, f"picked{g}", tag)
-            return picked[g]
-
-        def gather_step(g, j, c0=0, c1=S, tag=None):
-            nc.vector.tensor_copy(picked_tile(g, tag)[:, c0:c1, j], window(g, j, c0, c1))
-
-        def new_flat(key, count, width, dtype, tag=None):
-            flat[key] = sbuf([P, count, width], dtype, f"flat{key}", tag)
-
-        def gather_flat(engine, key, slot, g, j, c0=0, c1=S, at=0):
-            dst = flat[key][:, slot, at : at + c1 - c0]
+        def interleave(engine, dst, src, run=RUN):
+            dst = dst.rearrange("p (c r) j -> p c j r", r=run)
+            src = src.rearrange("p j (c r) -> p c j r", r=run)
             if engine == "scalar":
-                nc.scalar.activation(dst, window(g, j, c0, c1), COPY)
+                nc.scalar.copy(dst, src)
             else:
-                nc.vector.tensor_copy(dst, window(g, j, c0, c1))
+                nc.vector.tensor_copy(dst, src)
 
-        def weave_x(engine, key, g, j0, j1, c0=0, c1=S, run=RUN, tag=None):
-            dst = picked_tile(g, tag)[:, c0:c1, j0:j1].rearrange("p (c r) j -> p c j r", r=run)
-            copy(engine, dst, flat[key][:].rearrange("p j (c r) -> p c j r", r=run))
+        def quantise(src, name, width, tag=None):
+            codes = sbuf([P, width], U32, "codes_" + name, tag)
+            scales = sbuf([P, width], U8, "scales_" + name)
+            return codes, scales
 
-        def place_x(engine, key, g, j, c0, c1):
-            copy(engine, picked_tile(g)[:, c0:c1, j], flat[key][:, 0, :])
+        def quantise_into(codes, scales, src):
+            nc.vector.quantize_mx(out=codes.bitcast(FP8X4), scales=scales, in_=src.rearrange("p n j -> p (n j)"))
 
-        def quant_x(g, c0=0, c1=S, tag=None):
-            if g not in x_codes:
-                x_codes[g] = sbuf([P, S], U32, f"x_codes{g}", tag)
-                x_scales[g] = sbuf([P, S], U8, f"x_scales{g}")
-            nc.vector.quantize_mx(out=x_codes[g][:, c0:c1].bitcast(FP8X4), scales=x_scales[g][:, c0:c1],
-                                  in_=picked[g][:, c0:c1, :].rearrange("p s j -> p (s j)"))
+        x_mx, w_bf, w_mx, acc = {}, {}, {}, {}
 
-        w_bf, group_tile, w_codes, w_scales = {}, {}, {}, {}
+        def woven(i, g, tiles):
+            tile = sbuf([P, len(tiles) * P, PACK], BF16, f"w_bf{i}{g}{tiles[0]}")
+            for at, m in enumerate(tiles):
+                w_bf[i, g, m] = (tile, at * P)
 
-        def group(*members, tag=None):
-            tile = sbuf([P, len(members) * P, PACK], BF16, "w_bf" + "".join(str(v) for v in members[0]), tag)
-            group_tile[members] = tile
-            for at, member in enumerate(members):
-                w_bf[member] = tile[:, at * P : (at + 1) * P, :]
+        def weave(engine, i, g, m, c0=0, c1=P):
+            tile, at = w_bf[i, g, m]
+            dst, src = tile[:, at + c0 : at + c1, :], rows[i, g][:, :, m * P + c0 : m * P + c1]
+            if engine == "gpsimd":
+                nc.gpsimd.tensor_copy(dst, src.rearrange("p j c -> p c j"))
+            else:
+                interleave(engine, dst, src)
 
-        def weave(i, g, m, engine, c0=0, c1=P, tag=None):
-            if (i, g, m) not in w_bf:
-                group((i, g, m), tag=tag)
-            raw, at = w_raw[i, g, m]
-            dst = w_bf[i, g, m][:, c0:c1, :].rearrange("p (c r) j -> p c j r", r=RUN)
-            copy(engine, dst, raw[:, 0:PACK, at + c0 : at + c1].rearrange("p j (c r) -> p c j r", r=RUN))
+        def quantise_w(i, g, tiles):
+            tile, at = w_bf[i, g, tiles[0]]
+            width = len(tiles) * P
+            codes, scales = quantise(None, f"w{i}{g}{tiles[0]}", width)
+            quantise_into(codes[:], scales[:], tile[:, at : at + width, :])
+            for n, m in enumerate(tiles):
+                w_mx[i, g, m] = (codes[:, n * P : (n + 1) * P], scales[:, n * P : (n + 1) * P])
 
-        def quant(*members, tag=None, scale_tag=None):
-            name = "".join(str(v) for v in members[0])
-            codes = sbuf([P, len(members) * P], U32, "w_codes" + name, tag)
-            scales = sbuf([P, len(members) * P], U8, "w_scales" + name, scale_tag)
-            nc.vector.quantize_mx(out=codes[:].bitcast(FP8X4), scales=scales[:],
-                                  in_=group_tile[members][:].rearrange("p n j -> p (n j)"))
-            for at, member in enumerate(members):
-                w_codes[member] = codes[:, at * P : (at + 1) * P]
-                w_scales[member] = scales[:, at * P : (at + 1) * P]
-
-        acc, passes_done = {}, {}
+        def product(dst, w, x, c0, c1, start, stop):
+            nc.tensor.matmul_mx(out=dst, lhsT=w[0].bitcast(FP8X4), lhsT_scale=w[1], rhs=x[0][:, c0:c1].bitcast(FP8X4),
+                                rhs_scale=x[1][:, c0:c1], start=start, stop=stop)
 
         def mm(i, g, m, c0=0, c1=S, tag=None):
-            done = passes_done.get((i, m, c0), 0)
-            passes_done[i, m, c0] = done + 1
-            if done == 0:
+            if g == 0:
                 acc[i, m, c0] = psum.tile([P, c1 - c0], F32, name=f"acc{i}{m}{c0}", tag=tag or f"acc{i}{m}{c0}")
-            nc.tensor.matmul_mx(out=acc[i, m, c0][:], lhsT=w_codes[i, g, m].bitcast(FP8X4), lhsT_scale=w_scales[i, g, m],
-                                rhs=x_codes[g][:, c0:c1].bitcast(FP8X4), rhs_scale=x_scales[g][:, c0:c1],
-                                start=(done == 0), stop=(done == PASSES - 1))
+            product(acc[i, m, c0][:], w_mx[i, g, m], x_mx[g], c0, c1, g == 0, g == 1)
 
-        def warm_up(g, c0, c1, tag):
+        def halves(i, g, m, tags=(None, None)):
+            mm(i, g, m, 0, H, tags[0])
+            mm(i, g, m, H, S, tags[1])
+
+        def warm_up(c0, c1, tag):
             unread = psum.tile([P, c1 - c0], F32, name="unread", tag=tag)
-            nc.tensor.matmul_mx(out=unread[:], lhsT=w_codes[0, 0, 1].bitcast(FP8X4), lhsT_scale=w_scales[0, 0, 1],
-                                rhs=x_codes[g][:, c0:c1].bitcast(FP8X4), rhs_scale=x_scales[g][:, c0:c1], start=True, stop=True)
+            product(unread[:], w_mx[0, 0, 1], x_mx[1], c0, c1, True, True)
 
-        def bank(i, m, c0, c1):
-            start = max(k[2] for k in acc if k[:2] == (i, m) and k[2] <= c0)
-            return acc[i, m, start][:, c0 - start : c1 - start]
+        def shaped(ap, width):
+            if len(ap.shape) == 2:
+                return ap.rearrange("p (a b) -> p a b", b=width)
+            if ap.shape[2] == width:
+                return ap
+            return ap.rearrange("p a (c b) -> p a c b", b=width)
 
-        def rows_like(flat_ap, shaped):
-            if len(shaped.shape) == 2:
-                return flat_ap
-            return flat_ap.rearrange("p (a b) -> p a b", b=shaped.shape[2])
-
-        def piece(tiles, m, c0, c1):
-            start = max(k[1] for k in tiles if k[0] == m and k[1] <= c0)
-            whole = tiles[m, start]
-            if len(whole.shape) == 2:
-                return whole[:, c0 - start : c1 - start]
-            width = whole.shape[2]
-            return whole[:, (c0 - start) // width : (c1 - start) // width, :]
-
-        first, second = {}, {}
-
-        def evac(m, c0=0, c1=S, i=0, tag=None, into=None):
-            first[m, c0] = into if into is not None else sbuf([P, c1 - c0], F32, f"first{m}{c0}", tag)[:]
-            nc.scalar.copy(first[m, c0], rows_like(bank(i, m, c0, c1), first[m, c0]))
-
-        def minimum(dst, i, m, c0, c1, other):
-            width = min(dst.shape[-1], other.shape[-1])
-            views = []
-            for v in (dst, bank(i, m, c0, c1), other):
-                if len(v.shape) == 2 and width < v.shape[1]:
-                    v = v.rearrange("p (a b) -> p a b", b=width)
-                elif len(v.shape) == 3 and width < v.shape[2]:
-                    v = v.rearrange("p a (c b) -> p a c b", b=width)
-                views.append(v)
-            if max(len(v.shape) for v in views) == 4:
-                rows = [v.shape[1] for v in views if len(v.shape) == 4][0]
-                views = [v if len(v.shape) == 4 else v.rearrange("p (a c) b -> p a c b", a=rows) for v in views]
-            nc.vector.tensor_tensor(views[0], views[1], views[2], MIN)
-
-        def min2(m, c0=0, c1=S, i=1, tag=None, into=None):
-            second[m, c0] = into if into is not None else sbuf([P, c1 - c0], F32, f"second{m}{c0}", tag)[:]
-            minimum(second[m, c0], i, m, c0, c1, piece(first, m, c0, c1))
-
-        def min3(m, c0, c1, queue, i=2, tag=None, into=None):
-            result = into if into is not None else sbuf([P, c1 - c0], F32, f"result{m}{c0}", tag)[:]
-            minimum(result, i, m, c0, c1, piece(second, m, c0, c1))
-            queue.dma_start(out=out[m * P : (m + 1) * P, c0:c1], in_=result)
+        def minimum(dst, bank, other, width=None):
+            if width is not None:
+                dst, bank, other = shaped(dst, width), shaped(bank, width), shaped(other, width)
+            nc.vector.tensor_tensor(dst, bank, other, MIN)
 
         load_planes(0, 0, 4)
         nc.sync.dma_start(offsets[:], offs)
         load_planes(1, 0, 2)
         load_planes(1, 2, 3)
-        load_w(0, 0, 0, 2)
+        load_w(0, 0)
         load_planes(1, 3, 4)
-        load_w(0, 1, 0, 2)
-        load_w(1, 0, 0, 2, depth=8)
-        load_w(1, 1, 0, 2)
-        load_w(2, 0, 0, 2, depth=8)
-        load_w(2, 1, 0, 1)
-        load_w(2, 1, 1, 2)
-        new_flat("a", 4, S, F32)
-        gather_flat("scalar", "a", 3, 0, 3)
+        load_w(0, 1)
+        load_w(1, 0, after=4)
+        load_w(1, 1)
+        load_w(2, 0)
+        load_w(2, 1, before=1, after=3)
+
+        picked0 = sbuf([P, S, PACK], BF16, "picked0")
+        flat0 = sbuf([P, PACK, S], F32, "flat0")
+        nc.scalar.activation(flat0[:, 3, :], window(0, 3, 0, S), COPY)
         for j in range(3):
-            gather_flat("vector", "a", j, 0, j)
-        weave_x("vector", "a", 0, 0, 4)
-        quant_x(0)
-        new_flat("b", 2, S, F32)
-        gather_flat("scalar", "b", 0, 1, 0)
-        gather_flat("scalar", "b", 1, 1, 1, H, S, at=H)
-        gather_flat("vector", "b", 1, 1, 1, 0, H)
-        weave_x("vector", "b", 1, 0, 2, run=2)
-        new_flat("d", 1, S, BF16)
-        gather_flat("scalar", "d", 0, 1, 2)
-        place_x("vector", "d", 1, 2, 0, S)
-        group((0, 0, 0), (0, 0, 1))
-        weave(0, 0, 0, "scalar")
-        weave(0, 0, 1, "scalar")
-        quant((0, 0, 0), (0, 0, 1))
-        mm(0, 0, 0, 0, H)
-        mm(0, 0, 0, H, S)
+            nc.vector.tensor_copy(flat0[:, j, :], window(0, j, 0, S))
+        interleave("vector", picked0[:], flat0[:])
+        x_mx[0] = quantise(None, "x0", S)
+        quantise_into(x_mx[0][0][:], x_mx[0][1][:], picked0[:])
+
+        picked1 = sbuf([P, S, PACK], BF16, "picked1")
+        flat1 = sbuf([P, 2, S], F32, "flat1")
+        nc.scalar.activation(flat1[:, 0, :], window(1, 0, 0, S), COPY)
+        nc.scalar.activation(flat1[:, 1, H:S], window(1, 1, H, S), COPY)
+        nc.vector.tensor_copy(flat1[:, 1, 0:H], window(1, 1, 0, H))
+        interleave("vector", picked1[:, :, 0:2], flat1[:], run=2)
+        third = sbuf([P, S], BF16, "third")
+        nc.scalar.activation(third[:], window(1, 2, 0, S), COPY)
+        nc.vector.tensor_copy(picked1[:, :, 2], third[:])
+
+        woven(0, 0, (0, 1))
+        weave("scalar", 0, 0, 0)
+        weave("scalar", 0, 0, 1)
+        quantise_w(0, 0, (0, 1))
+        halves(0, 0, 0)
         mm(0, 0, 1)
-        new_flat("c", 1, H, BF16)
-        gather_flat("scalar", "c", 0, 1, 3, H, S)
-        gather_step(1, 3, 0, H)
-        place_x("vector", "c", 1, 3, H, S)
-        quant_x(1, 0, H, tag="plane13")
-        quant_x(1, H, S)
-        warm_up(1, 0, H, "acc200")
-        warm_up(1, H, S, "acc20256")
-        weave(0, 1, 0, "scalar")
-        weave(0, 1, 1, "scalar")
-        quant((0, 1, 0))
-        mm(0, 1, 0, 0, H)
-        mm(0, 1, 0, H, S)
-        group((1, 0, 0), (1, 0, 1))
-        weave(1, 0, 0, "vector")
-        weave(1, 0, 1, "scalar")
-        quant((0, 1, 1))
+
+        fourth = sbuf([P, H], BF16, "fourth")
+        nc.scalar.activation(fourth[:], window(1, 3, H, S), COPY)
+        nc.vector.tensor_copy(picked1[:, 0:H, 3], window(1, 3, 0, H))
+        nc.vector.tensor_copy(picked1[:, H:S, 3], fourth[:])
+        x_mx[1] = quantise(None, "x1", S, tag="plane13")
+        quantise_into(x_mx[1][0][:, 0:H], x_mx[1][1][:, 0:H], picked1[:, 0:H, :])
+        quantise_into(x_mx[1][0][:, H:S], x_mx[1][1][:, H:S], picked1[:, H:S, :])
+        warm_up(0, H, "acc200")
+        warm_up(H, S, "acc20256")
+
+        woven(0, 1, (0,))
+        woven(0, 1, (1,))
+        weave("scalar", 0, 1, 0)
+        weave("scalar", 0, 1, 1)
+        quantise_w(0, 1, (0,))
+        halves(0, 1, 0)
+        woven(1, 0, (0, 1))
+        weave("vector", 1, 0, 0)
+        weave("scalar", 1, 0, 1)
+        quantise_w(0, 1, (1,))
         mm(0, 1, 1)
-        quant((1, 0, 0), (1, 0, 1))
-        mm(1, 0, 0, 0, H)
-        mm(1, 0, 0, H, S)
+        quantise_w(1, 0, (0, 1))
+        halves(1, 0, 0)
         mm(1, 0, 1)
-        raw2 = w_raw[1, 0, 0][0]
-        evac(0, 0, H, into=raw2[:, 0:8:2, 0:64])
-        evac(0, H, S, into=raw2[:, 1:8:2, 0:64])
-        evac(1, into=raw2[:, :, 64:P])
-        weave(1, 1, 0, "vector")
-        weave(1, 1, 1, "vector")
-        quant((1, 1, 0))
-        quant((1, 1, 1))
-        mm(1, 1, 0, 0, H)
-        mm(1, 1, 0, H, S)
+
+        first = {(0, 0): raw[1, 0][:, 0:8:2, 0:64], (0, H): raw[1, 0][:, 1:8:2, 0:64]}
+        whole = raw[1, 0][:, :, 64:P]
+        first[1, 0], first[1, H] = whole[:, 0:4, :], whole[:, 4:8, :]
+        nc.scalar.copy(first[0, 0], shaped(acc[0, 0, 0][:], 64))
+        nc.scalar.copy(first[0, H], shaped(acc[0, 0, H][:], 64))
+        nc.scalar.copy(whole, shaped(acc[0, 1, 0][:], 64))
+
+        POOL_FROM = 128
+        shared = sbuf([P, POOL_FROM + P, PACK], BF16, "w_bf20")
+        woven(1, 1, (0,))
+        w_bf[1, 1, 1] = (shared, POOL_FROM)
+        weave("vector", 1, 1, 0)
+        weave("vector", 1, 1, 1)
+        quantise_w(1, 1, (0,))
+        quantise_w(1, 1, (1,))
+        halves(1, 1, 0)
         mm(1, 1, 1)
-        group((2, 0, 0), (2, 0, 1))
-        raw3 = w_raw[2, 0, 0][0]
-        weave(2, 0, 1, "vector")
-        weave(2, 0, 0, "scalar", 0, 64)
-        weave(2, 0, 0, "scalar", 64, P)
-        min2(0, 0, H, into=raw3[:, 0:8:2, 0:64])
-        min2(0, H, S, into=raw3[:, 1:8:2, 0:64])
-        quant((2, 0, 0), (2, 0, 1))
-        mm(2, 0, 0, 0, H)
-        mm(2, 0, 0, H, S)
-        mm(2, 0, 1, 0, H, tag="acc000")
-        mm(2, 0, 1, H, S, tag="acc00256")
-        min2(1, 0, H, into=raw3[:, 0:PACK, 64:P])
-        weave(2, 1, 0, "scalar")
-        quant((2, 1, 0))
-        mm(2, 1, 0, 0, H)
-        mm(2, 1, 0, H, S)
-        min2(1, H, S, tag="w_raw210")
-        weave(2, 1, 1, "scalar")
-        quant((2, 1, 1))
-        mm(2, 1, 1, 0, H)
-        mm(2, 1, 1, H, S)
-        last = w_raw[2, 1, 1][0][:].rearrange("p j n -> p (j n)")
-        min3(0, 0, H, nc.sync, into=last[:, 0:H])
-        min3(0, H, S, nc.sync, into=last[:, H:S])
-        min3(1, 0, H, nc.sync)
-        min3(1, H, S, nc.sync)
+
+        second = {}
+        w_bf[2, 0, 0], w_bf[2, 0, 1] = (shared, 0), (shared, P)
+        weave("scalar", 2, 0, 0, 0, POOL_FROM)
+        weave("gpsimd", 2, 0, 0, POOL_FROM, N)
+        for c0 in (0, H):
+            second[0, c0] = sbuf([P, H], F32, f"second0{c0}")[:]
+            minimum(second[0, c0], acc[1, 0, c0][:], first[0, c0], 64)
+        quantise_w(2, 0, (0, 1))
+        halves(2, 0, 0)
+        halves(2, 0, 1, ("acc000", "acc00256"))
+
+        last = raw[2, 1][:].rearrange("p j n -> p (j n)")
+        HELD, SHARE = 16, 80
+        woven(2, 1, (0,))
+        woven(2, 1, (1,))
+        weave("scalar", 2, 1, 0, 0, HELD)
+        weave("vector", 2, 1, 0, SHARE, P)
+        weave("scalar", 2, 1, 0, HELD, SHARE)
+        second[1, 0] = last[:, HELD : HELD + H]
+        minimum(second[1, 0], acc[1, 1, 0][:, 0:H], first[1, 0], 64)
+        quantise_w(2, 1, (0,))
+        halves(2, 1, 0)
+        second[1, H] = raw[2, 1][:, 4:8, HELD : HELD + 64]
+        minimum(second[1, H], acc[1, 1, 0][:, H:S], first[1, H], 64)
+        weave("scalar", 2, 1, 1)
+        quantise_w(2, 1, (1,))
+        halves(2, 1, 1)
+
+        for m in range(2):
+            for n, c0 in enumerate((0, H)):
+                if m == 0:
+                    result = last[:, N + P + n * H : N + P + (n + 1) * H]
+                else:
+                    result = sbuf([P, H], F32, f"result{c0}")[:]
+                minimum(result, acc[2, m, c0][:], second[m, c0], 64 if (m, c0) == (1, H) else None)
+                nc.sync.dma_start(out=out[m * P : (m + 1) * P, c0 : c0 + H], in_=result)

@@ -12,6 +12,8 @@ U16 = mybir.dt.uint16
 U8 = mybir.dt.uint8
 FP8X4 = mybir.dt.float8_e4m3fn_x4
 MIN = mybir.AluOpType.min
+MULT = mybir.AluOpType.mult
+ADD = mybir.AluOpType.add
 COPY = mybir.ActivationFunctionType.Copy
 
 P = 128
@@ -27,9 +29,12 @@ def tile_picked_maxout_min_e_kernel(tc, xT, w1, w2, w3, offs, out):
     weights = (w1, w2, w3)
     with ExitStack() as ctx:
         keep = ctx.enter_context(tc.tile_pool(name="keep", bufs=1))
+        turns = ctx.enter_context(tc.tile_pool(name="turns", bufs=1))
         psum = ctx.enter_context(tc.psum_pool(name="psum", bufs=1))
 
-        def sbuf(shape, dtype, name, tag=None):
+        def sbuf(shape, dtype, name, tag=None, at=None):
+            if at is not None:
+                return turns.tile(shape, dtype, name=name, tag=name, align_bytes=ALIGN, offset=at)
             return keep.tile(shape, dtype, name=name, tag=tag or name, align_bytes=ALIGN)
 
         offsets = keep.tile([P, S // 16], U16, name="offsets")
@@ -42,12 +47,14 @@ def tile_picked_maxout_min_e_kernel(tc, xT, w1, w2, w3, offs, out):
             for j in range(j0, j1):
                 planes[g, j] = tile[:, (j - j0) * T : (j - j0 + 1) * T]
 
-        def load_w(i, g, before=0, after=0):
-            tile = sbuf([P, before + PACK + after, N], F32, f"w_raw{i}{g}")
-            src = weights[i][g * K_PASS : (g + 1) * K_PASS, :].rearrange("(p j) n -> p j n", j=PACK)
-            nc.sync.dma_start(out=tile[:, before : before + PACK, :], in_=src)
-            raw[i, g] = tile
-            rows[i, g] = tile[:, before : before + PACK, :]
+        def load_w(i, g, tiles=(0, 1), after=0, at=None):
+            tile = sbuf([P, PACK + after, len(tiles) * P], F32, f"w_raw{i}{g}{tiles[0]}", at=at)
+            cols = slice(tiles[0] * P, (tiles[-1] + 1) * P)
+            src = weights[i][g * K_PASS : (g + 1) * K_PASS, cols].rearrange("(p j) n -> p j n", j=PACK)
+            nc.sync.dma_start(out=tile[:, 0:PACK, :], in_=src)
+            for at, m in enumerate(tiles):
+                raw[i, g, m] = tile
+                rows[i, g, m] = tile[:, 0:PACK, at * P :]
 
         def window(g, j, c0, c1):
             return planes[g, j].indirect(offsets[:, c0 // 16 : c1 // 16])
@@ -60,8 +67,8 @@ def tile_picked_maxout_min_e_kernel(tc, xT, w1, w2, w3, offs, out):
             else:
                 nc.vector.tensor_copy(dst, src)
 
-        def quantise(src, name, width, tag=None):
-            codes = sbuf([P, width], U32, "codes_" + name, tag)
+        def quantise(src, name, width, tag=None, at=None):
+            codes = sbuf([P, width], U32, "codes_" + name, tag, at)
             scales = sbuf([P, width], U8, "scales_" + name)
             return codes, scales
 
@@ -77,16 +84,16 @@ def tile_picked_maxout_min_e_kernel(tc, xT, w1, w2, w3, offs, out):
 
         def weave(engine, i, g, m, c0=0, c1=P):
             tile, at = w_bf[i, g, m]
-            dst, src = tile[:, at + c0 : at + c1, :], rows[i, g][:, :, m * P + c0 : m * P + c1]
+            dst, src = tile[:, at + c0 : at + c1, :], rows[i, g, m][:, :, c0:c1]
             if engine == "gpsimd":
-                nc.gpsimd.tensor_copy(dst, src.rearrange("p j c -> p c j"))
+                nc.gpsimd.tensor_scalar(dst, src.rearrange("p j c -> p c j"), 1.0, 0.0, MULT, ADD)
             else:
                 interleave(engine, dst, src)
 
-        def quantise_w(i, g, tiles):
+        def quantise_w(i, g, tiles, place=None):
             tile, at = w_bf[i, g, tiles[0]]
             width = len(tiles) * P
-            codes, scales = quantise(None, f"w{i}{g}{tiles[0]}", width)
+            codes, scales = quantise(None, f"w{i}{g}{tiles[0]}", width, at=place)
             quantise_into(codes[:], scales[:], tile[:, at : at + width, :])
             for n, m in enumerate(tiles):
                 w_mx[i, g, m] = (codes[:, n * P : (n + 1) * P], scales[:, n * P : (n + 1) * P])
@@ -130,7 +137,8 @@ def tile_picked_maxout_min_e_kernel(tc, xT, w1, w2, w3, offs, out):
         load_w(1, 0, after=4)
         load_w(1, 1)
         load_w(2, 0)
-        load_w(2, 1, before=1, after=3)
+        load_w(2, 1, (0,), at=0)
+        load_w(2, 1, (1,))
 
         picked0 = sbuf([P, S, PACK], BF16, "picked0")
         flat0 = sbuf([P, PACK, S], F32, "flat0")
@@ -183,8 +191,8 @@ def tile_picked_maxout_min_e_kernel(tc, xT, w1, w2, w3, offs, out):
         halves(1, 0, 0)
         mm(1, 0, 1)
 
-        first = {(0, 0): raw[1, 0][:, 0:8:2, 0:64], (0, H): raw[1, 0][:, 1:8:2, 0:64]}
-        whole = raw[1, 0][:, :, 64:P]
+        first = {(0, 0): raw[1, 0, 0][:, 0:8:2, 0:64], (0, H): raw[1, 0, 0][:, 1:8:2, 0:64]}
+        whole = raw[1, 0, 0][:, :, 64:P]
         first[1, 0], first[1, H] = whole[:, 0:4, :], whole[:, 4:8, :]
         nc.scalar.copy(first[0, 0], shaped(acc[0, 0, 0][:], 64))
         nc.scalar.copy(first[0, H], shaped(acc[0, 0, H][:], 64))
@@ -205,35 +213,29 @@ def tile_picked_maxout_min_e_kernel(tc, xT, w1, w2, w3, offs, out):
         w_bf[2, 0, 0], w_bf[2, 0, 1] = (shared, 0), (shared, P)
         weave("scalar", 2, 0, 0, 0, POOL_FROM)
         weave("gpsimd", 2, 0, 0, POOL_FROM, N)
-        for c0 in (0, H):
-            second[0, c0] = sbuf([P, H], F32, f"second0{c0}")[:]
-            minimum(second[0, c0], acc[1, 0, c0][:], first[0, c0], 64)
-        quantise_w(2, 0, (0, 1))
+        for m, c0 in ((0, 0), (0, H), (1, 0)):
+            second[m, c0] = sbuf([P, H], F32, f"second{m}{c0}")[:]
+            bank = acc[1, 0, c0][:] if m == 0 else acc[1, 1, 0][:, c0 : c0 + H]
+            minimum(second[m, c0], bank, first[m, c0], 64)
+        quantise_w(2, 0, (0,))
         halves(2, 0, 0)
-        halves(2, 0, 1, ("acc000", "acc00256"))
 
-        last = raw[2, 1][:].rearrange("p j n -> p (j n)")
-        HELD, SHARE = 16, 80
         woven(2, 1, (0,))
         woven(2, 1, (1,))
-        weave("scalar", 2, 1, 0, 0, HELD)
-        weave("vector", 2, 1, 0, SHARE, P)
-        weave("scalar", 2, 1, 0, HELD, SHARE)
-        second[1, 0] = last[:, HELD : HELD + H]
-        minimum(second[1, 0], acc[1, 1, 0][:, 0:H], first[1, 0], 64)
+        weave("scalar", 2, 1, 0)
         quantise_w(2, 1, (0,))
         halves(2, 1, 0)
-        second[1, H] = raw[2, 1][:, 4:8, HELD : HELD + 64]
+        second[1, H] = sbuf([P, H], F32, "second1h", at=0)[:]
         minimum(second[1, H], acc[1, 1, 0][:, H:S], first[1, H], 64)
+        quantise_w(2, 0, (1,), place=4 * H)
+        halves(2, 0, 1, ("acc000", "acc00256"))
         weave("scalar", 2, 1, 1)
         quantise_w(2, 1, (1,))
         halves(2, 1, 1)
 
+        last = raw[2, 1, 1][:].rearrange("p j n -> p (j n)")
         for m in range(2):
-            for n, c0 in enumerate((0, H)):
-                if m == 0:
-                    result = last[:, N + P + n * H : N + P + (n + 1) * H]
-                else:
-                    result = sbuf([P, H], F32, f"result{c0}")[:]
-                minimum(result, acc[2, m, c0][:], second[m, c0], 64 if (m, c0) == (1, H) else None)
+            for c0 in (0, H):
+                result = last[:, c0 : c0 + H] if m == 0 else sbuf([P, H], F32, f"result{c0}")[:]
+                minimum(result, acc[2, m, c0][:], second[m, c0])
                 nc.sync.dma_start(out=out[m * P : (m + 1) * P, c0 : c0 + H], in_=result)

@@ -21,6 +21,7 @@ PACK = 4
 K_PASS = P * PACK
 RUN = 4
 H = S // 2
+Q = S // 4
 ALIGN = 256
 
 
@@ -111,6 +112,10 @@ def tile_picked_maxout_min_e_kernel(tc, xT, w1, w2, w3, offs, out):
             mm(i, g, m, 0, H, tags[0])
             mm(i, g, m, H, S, tags[1])
 
+        def pieces(i, g, tags=(None, None, None)):
+            for (c0, c1), tag in zip(((0, Q), (Q, H), (H, S)), tags):
+                mm(i, g, 0, c0, c1, tag)
+
         def warm_up(c0, c1, tag):
             unread = psum.tile([P, c1 - c0], F32, name="unread", tag=tag)
             product(unread[:], w_mx[0, 0, 1], x_mx[1], c0, c1, True, True)
@@ -173,8 +178,8 @@ def tile_picked_maxout_min_e_kernel(tc, xT, w1, w2, w3, offs, out):
         x_mx[1] = quantise(None, "x1", S, tag="plane13")
         quantise_into(x_mx[1][0][:, 0:H], x_mx[1][1][:, 0:H], picked1[:, 0:H, :])
         quantise_into(x_mx[1][0][:, H:S], x_mx[1][1][:, H:S], picked1[:, H:S, :])
-        warm_up(0, H, "acc200")
-        warm_up(H, S, "acc20256")
+        warm_up(0, H, "acc100")
+        warm_up(H, S, "acc10256")
 
         woven(0, 1, (0,))
         woven(0, 1, (1,))
@@ -188,7 +193,7 @@ def tile_picked_maxout_min_e_kernel(tc, xT, w1, w2, w3, offs, out):
         quantise_w(0, 1, (1,))
         mm(0, 1, 1)
         quantise_w(1, 0, (0, 1))
-        halves(1, 0, 0)
+        pieces(1, 0)
         mm(1, 0, 1)
 
         first = {(0, 0): raw[1, 0, 0][:, 0:8:2, 0:64], (0, H): raw[1, 0, 0][:, 1:8:2, 0:64]}
@@ -200,13 +205,13 @@ def tile_picked_maxout_min_e_kernel(tc, xT, w1, w2, w3, offs, out):
 
         POOL_FROM = 128
         shared = sbuf([P, POOL_FROM + P, PACK], BF16, "w_bf20")
-        woven(1, 1, (0,))
-        w_bf[1, 1, 1] = (shared, POOL_FROM)
+        woven(1, 1, (1,))
+        w_bf[1, 1, 0] = (shared, POOL_FROM)
         weave("vector", 1, 1, 0)
         weave("vector", 1, 1, 1)
         quantise_w(1, 1, (0,))
         quantise_w(1, 1, (1,))
-        halves(1, 1, 0)
+        pieces(1, 1)
         mm(1, 1, 1)
 
         second = {}
@@ -215,20 +220,22 @@ def tile_picked_maxout_min_e_kernel(tc, xT, w1, w2, w3, offs, out):
         weave("gpsimd", 2, 0, 0, POOL_FROM, N)
         for m, c0 in ((0, 0), (0, H), (1, 0)):
             second[m, c0] = sbuf([P, H], F32, f"second{m}{c0}")[:]
-            bank = acc[1, 0, c0][:] if m == 0 else acc[1, 1, 0][:, c0 : c0 + H]
-            minimum(second[m, c0], bank, first[m, c0], 64)
+        minimum(second[0, 0][:, 0:Q], acc[1, 0, 0][:], first[0, 0][:, 0:2, :], 64)
+        minimum(second[0, 0][:, Q:H], acc[1, 0, Q][:], first[0, 0][:, 2:4, :], 64)
+        minimum(second[0, H], acc[1, 0, H][:], first[0, H], 64)
+        minimum(second[1, 0], acc[1, 1, 0][:, 0:H], first[1, 0], 64)
         quantise_w(2, 0, (0,))
-        halves(2, 0, 0)
+        pieces(2, 0, ("acc200", "acc000", "acc00256"))
 
         woven(2, 1, (0,))
         woven(2, 1, (1,))
         weave("scalar", 2, 1, 0)
         quantise_w(2, 1, (0,))
-        halves(2, 1, 0)
+        pieces(2, 1)
         second[1, H] = sbuf([P, H], F32, "second1h", at=0)[:]
         minimum(second[1, H], acc[1, 1, 0][:, H:S], first[1, H], 64)
         quantise_w(2, 0, (1,), place=4 * H)
-        halves(2, 0, 1, ("acc000", "acc00256"))
+        halves(2, 0, 1, ("acc010", "acc100"))
         weave("scalar", 2, 1, 1)
         quantise_w(2, 1, (1,))
         halves(2, 1, 1)
@@ -237,5 +244,9 @@ def tile_picked_maxout_min_e_kernel(tc, xT, w1, w2, w3, offs, out):
         for m in range(2):
             for c0 in (0, H):
                 result = last[:, c0 : c0 + H] if m == 0 else sbuf([P, H], F32, f"result{c0}")[:]
-                minimum(result, acc[2, m, c0][:], second[m, c0])
+                if (m, c0) == (0, 0):
+                    minimum(result[:, 0:Q], acc[2, 0, 0][:], second[0, 0][:, 0:Q])
+                    minimum(result[:, Q:H], acc[2, 0, Q][:], second[0, 0][:, Q:H])
+                else:
+                    minimum(result, acc[2, m, c0][:], second[m, c0])
                 nc.sync.dma_start(out=out[m * P : (m + 1) * P, c0 : c0 + H], in_=result)

@@ -203,10 +203,10 @@ def tile_picked_maxout_min_e_kernel(tc, xT, w1, w2, w3, offs, out):
         nc.scalar.copy(first[0, H], shaped(acc[0, 0, H][:], 64))
         nc.scalar.copy(whole, shaped(acc[0, 1, 0][:], 64))
 
-        POOL_FROM = 128
-        shared = sbuf([P, POOL_FROM + P, PACK], BF16, "w_bf20")
+        LEAD = 96
+        shared = sbuf([P, LEAD + N, PACK], BF16, "w_bf20")
         woven(1, 1, (1,))
-        w_bf[1, 1, 0] = (shared, POOL_FROM)
+        w_bf[1, 1, 0] = (shared, LEAD + P)
         weave("vector", 1, 1, 0)
         weave("vector", 1, 1, 1)
         quantise_w(1, 1, (0,))
@@ -215,9 +215,9 @@ def tile_picked_maxout_min_e_kernel(tc, xT, w1, w2, w3, offs, out):
         mm(1, 1, 1)
 
         second = {}
-        w_bf[2, 0, 0], w_bf[2, 0, 1] = (shared, 0), (shared, P)
-        weave("scalar", 2, 0, 0, 0, POOL_FROM)
-        weave("gpsimd", 2, 0, 0, POOL_FROM, N)
+        w_bf[2, 0, 0], w_bf[2, 0, 1] = (shared, LEAD), (shared, LEAD + P)
+        weave("scalar", 2, 0, 0)
+        weave("gpsimd", 2, 0, 1)
         for m, c0 in ((0, 0), (0, H), (1, 0)):
             second[m, c0] = sbuf([P, H], F32, f"second{m}{c0}")[:]
         minimum(second[0, 0][:, 0:Q], acc[1, 0, 0][:], first[0, 0][:, 0:2, :], 64)
@@ -227,16 +227,19 @@ def tile_picked_maxout_min_e_kernel(tc, xT, w1, w2, w3, offs, out):
         quantise_w(2, 0, (0,))
         pieces(2, 0, ("acc200", "acc000", "acc00256"))
 
+        POOL_SHARE = 32
         woven(2, 1, (0,))
-        woven(2, 1, (1,))
-        weave("scalar", 2, 1, 0)
+        weave("gpsimd", 2, 1, 0, P - POOL_SHARE, P)
+        weave("scalar", 2, 1, 0, 0, P - POOL_SHARE)
         quantise_w(2, 1, (0,))
         pieces(2, 1)
         second[1, H] = sbuf([P, H], F32, "second1h", at=0)[:]
         minimum(second[1, H], acc[1, 1, 0][:, H:S], first[1, H], 64)
         quantise_w(2, 0, (1,), place=4 * H)
         halves(2, 0, 1, ("acc010", "acc100"))
-        weave("scalar", 2, 1, 1)
+        w_bf[2, 1, 1] = (shared, 0)
+        weave("gpsimd", 2, 1, 1, P - POOL_SHARE, P)
+        weave("scalar", 2, 1, 1, 0, P - POOL_SHARE)
         quantise_w(2, 1, (1,))
         halves(2, 1, 1)
 

from contextlib import ExitStack

import concourse.mybir as mybir

K, T, S, N = 1024, 2048, 512, 256
FLOPS = 3 * 2 * K * S * N

F32 = mybir.dt.float32
BF16 = mybir.dt.bfloat16
U32 = mybir.dt.uint32
U16 = mybir.dt.uint16
U8 = mybir.dt.uint8
FP8X4 = mybir.dt.float8_e4m3fn_x4
MIN = mybir.AluOpType.min
MULT = mybir.AluOpType.mult
ADD = mybir.AluOpType.add
COPY = mybir.ActivationFunctionType.Copy

P = 128
PACK = 4
K_PASS = P * PACK
RUN = 4
H = S // 2
Q = S // 4
ALIGN = 256


def tile_picked_maxout_min_e_kernel(tc, xT, w1, w2, w3, offs, out):
    nc = tc.nc
    weights = (w1, w2, w3)
    with ExitStack() as ctx:
        keep = ctx.enter_context(tc.tile_pool(name="keep", bufs=1))
        turns = ctx.enter_context(tc.tile_pool(name="turns", bufs=1))
        psum = ctx.enter_context(tc.psum_pool(name="psum", bufs=1))

        def sbuf(shape, dtype, name, tag=None, at=None):
            if at is not None:
                return turns.tile(shape, dtype, name=name, tag=name, align_bytes=ALIGN, offset=at)
            return keep.tile(shape, dtype, name=name, tag=tag or name, align_bytes=ALIGN)

        offsets = keep.tile([P, S // 16], U16, name="offsets")
        planes, raw, rows = {}, {}, {}

        def load_planes(g, j0, j1):
            tile = sbuf([P, (j1 - j0) * T], F32, f"plane{g}{j0}")
            src = xT[g * K_PASS : (g + 1) * K_PASS, :].rearrange("(p j) t -> p (j t)", j=PACK)
            nc.sync.dma_start(out=tile[:], in_=src[:, j0 * T : j1 * T])
            for j in range(j0, j1):
                planes[g, j] = tile[:, (j - j0) * T : (j - j0 + 1) * T]

        def load_w(i, g, tiles=(0, 1), after=0, at=None):
            tile = sbuf([P, PACK + after, len(tiles) * P], F32, f"w_raw{i}{g}{tiles[0]}", at=at)
            cols = slice(tiles[0] * P, (tiles[-1] + 1) * P)
            src = weights[i][g * K_PASS : (g + 1) * K_PASS, cols].rearrange("(p j) n -> p j n", j=PACK)
            nc.sync.dma_start(out=tile[:, 0:PACK, :], in_=src)
            for at, m in enumerate(tiles):
                raw[i, g, m] = tile
                rows[i, g, m] = tile[:, 0:PACK, at * P :]

        def window(g, j, c0, c1):
            return planes[g, j].indirect(offsets[:, c0 // 16 : c1 // 16])

        def interleave(engine, dst, src, run=RUN):
            dst = dst.rearrange("p (c r) j -> p c j r", r=run)
            src = src.rearrange("p j (c r) -> p c j r", r=run)
            if engine == "scalar":
                nc.scalar.copy(dst, src)
            else:
                nc.vector.tensor_copy(dst, src)

        def quantise(src, name, width, tag=None, at=None):
            codes = sbuf([P, width], U32, "codes_" + name, tag, at)
            scales = sbuf([P, width], U8, "scales_" + name)
            return codes, scales

        def quantise_into(codes, scales, src):
            nc.vector.quantize_mx(out=codes.bitcast(FP8X4), scales=scales, in_=src.rearrange("p n j -> p (n j)"))

        x_mx, w_bf, w_mx, acc = {}, {}, {}, {}

        def woven(i, g, tiles):
            tile = sbuf([P, len(tiles) * P, PACK], BF16, f"w_bf{i}{g}{tiles[0]}")
            for at, m in enumerate(tiles):
                w_bf[i, g, m] = (tile, at * P)

        def weave(engine, i, g, m, c0=0, c1=P):
            tile, at = w_bf[i, g, m]
            dst, src = tile[:, at + c0 : at + c1, :], rows[i, g, m][:, :, c0:c1]
            if engine == "gpsimd":
                nc.gpsimd.tensor_scalar(dst, src.rearrange("p j c -> p c j"), 1.0, 0.0, MULT, ADD)
            else:
                interleave(engine, dst, src)

        def quantise_w(i, g, tiles, place=None):
            tile, at = w_bf[i, g, tiles[0]]
            width = len(tiles) * P
            codes, scales = quantise(None, f"w{i}{g}{tiles[0]}", width, at=place)
            quantise_into(codes[:], scales[:], tile[:, at : at + width, :])
            for n, m in enumerate(tiles):
                w_mx[i, g, m] = (codes[:, n * P : (n + 1) * P], scales[:, n * P : (n + 1) * P])

        def product(dst, w, x, c0, c1, start, stop):
            nc.tensor.matmul_mx(out=dst, lhsT=w[0].bitcast(FP8X4), lhsT_scale=w[1], rhs=x[0][:, c0:c1].bitcast(FP8X4),
                                rhs_scale=x[1][:, c0:c1], start=start, stop=stop)

        def mm(i, g, m, c0=0, c1=S, tag=None):
            if g == 0:
                acc[i, m, c0] = psum.tile([P, c1 - c0], F32, name=f"acc{i}{m}{c0}", tag=tag or f"acc{i}{m}{c0}")
            product(acc[i, m, c0][:], w_mx[i, g, m], x_mx[g], c0, c1, g == 0, g == 1)

        def halves(i, g, m, tags=(None, None)):
            mm(i, g, m, 0, H, tags[0])
            mm(i, g, m, H, S, tags[1])

        def pieces(i, g, tags=(None, None, None)):
            for (c0, c1), tag in zip(((0, Q), (Q, H), (H, S)), tags):
                mm(i, g, 0, c0, c1, tag)

        def warm_up(c0, c1, tag):
            unread = psum.tile([P, c1 - c0], F32, name="unread", tag=tag)
            product(unread[:], w_mx[0, 0, 1], x_mx[1], c0, c1, True, True)

        def shaped(ap, width):
            if len(ap.shape) == 2:
                return ap.rearrange("p (a b) -> p a b", b=width)
            if ap.shape[2] == width:
                return ap
            return ap.rearrange("p a (c b) -> p a c b", b=width)

        def minimum(dst, bank, other, width=None):
            if width is not None:
                dst, bank, other = shaped(dst, width), shaped(bank, width), shaped(other, width)
            nc.vector.tensor_tensor(dst, bank, other, MIN)

        load_planes(0, 0, 4)
        nc.sync.dma_start(offsets[:], offs)
        load_planes(1, 0, 2)
        load_planes(1, 2, 3)
        load_w(0, 0)
        load_planes(1, 3, 4)
        load_w(0, 1)
        load_w(1, 0, after=4)
        load_w(1, 1)
        load_w(2, 0)
        load_w(2, 1, (0,), at=0)
        load_w(2, 1, (1,))

        picked0 = sbuf([P, S, PACK], BF16, "picked0")
        flat0 = sbuf([P, PACK, S], F32, "flat0")
        nc.scalar.activation(flat0[:, 3, :], window(0, 3, 0, S), COPY)
        for j in range(3):
            nc.vector.tensor_copy(flat0[:, j, :], window(0, j, 0, S))
        interleave("vector", picked0[:], flat0[:])
        x_mx[0] = quantise(None, "x0", S)
        quantise_into(x_mx[0][0][:], x_mx[0][1][:], picked0[:])

        picked1 = sbuf([P, S, PACK], BF16, "picked1")
        flat1 = sbuf([P, 2, S], F32, "flat1")
        nc.scalar.activation(flat1[:, 0, :], window(1, 0, 0, S), COPY)
        nc.scalar.activation(flat1[:, 1, H:S], window(1, 1, H, S), COPY)
        nc.vector.tensor_copy(flat1[:, 1, 0:H], window(1, 1, 0, H))
        interleave("vector", picked1[:, :, 0:2], flat1[:], run=2)
        third = sbuf([P, S], BF16, "third")
        nc.scalar.activation(third[:], window(1, 2, 0, S), COPY)
        nc.vector.tensor_copy(picked1[:, :, 2], third[:])

        woven(0, 0, (0, 1))
        weave("scalar", 0, 0, 0)
        weave("scalar", 0, 0, 1)
        quantise_w(0, 0, (0, 1))
        halves(0, 0, 0)
        mm(0, 0, 1)

        fourth = sbuf([P, H], BF16, "fourth")
        nc.scalar.activation(fourth[:], window(1, 3, H, S), COPY)
        nc.vector.tensor_copy(picked1[:, 0:H, 3], window(1, 3, 0, H))
        nc.vector.tensor_copy(picked1[:, H:S, 3], fourth[:])
        x_mx[1] = quantise(None, "x1", S, tag="plane13")
        quantise_into(x_mx[1][0][:, 0:H], x_mx[1][1][:, 0:H], picked1[:, 0:H, :])
        quantise_into(x_mx[1][0][:, H:S], x_mx[1][1][:, H:S], picked1[:, H:S, :])
        warm_up(0, H, "acc100")
        warm_up(H, S, "acc10256")

        woven(0, 1, (0,))
        woven(0, 1, (1,))
        weave("scalar", 0, 1, 0)
        weave("scalar", 0, 1, 1)
        quantise_w(0, 1, (0,))
        halves(0, 1, 0)
        woven(1, 0, (0, 1))
        weave("vector", 1, 0, 0)
        weave("scalar", 1, 0, 1)
        quantise_w(0, 1, (1,))
        mm(0, 1, 1)
        quantise_w(1, 0, (0, 1))
        pieces(1, 0)
        mm(1, 0, 1)

        first = {(0, 0): raw[1, 0, 0][:, 0:8:2, 0:64], (0, H): raw[1, 0, 0][:, 1:8:2, 0:64]}
        whole = raw[1, 0, 0][:, :, 64:P]
        first[1, 0], first[1, H] = whole[:, 0:4, :], whole[:, 4:8, :]
        nc.scalar.copy(first[0, 0], shaped(acc[0, 0, 0][:], 64))
        nc.scalar.copy(first[0, H], shaped(acc[0, 0, H][:], 64))
        nc.scalar.copy(whole, shaped(acc[0, 1, 0][:], 64))

        LEAD = 96
        shared = sbuf([P, LEAD + N, PACK], BF16, "w_bf20")
        woven(1, 1, (1,))
        w_bf[1, 1, 0] = (shared, LEAD + P)
        weave("vector", 1, 1, 0)
        weave("vector", 1, 1, 1)
        quantise_w(1, 1, (0,))
        quantise_w(1, 1, (1,))
        pieces(1, 1)
        mm(1, 1, 1)

        second = {}
        w_bf[2, 0, 0], w_bf[2, 0, 1] = (shared, LEAD), (shared, LEAD + P)
        weave("scalar", 2, 0, 0)
        weave("gpsimd", 2, 0, 1)
        for m, c0 in ((0, 0), (0, H), (1, 0)):
            second[m, c0] = sbuf([P, H], F32, f"second{m}{c0}")[:]
        minimum(second[0, 0][:, 0:Q], acc[1, 0, 0][:], first[0, 0][:, 0:2, :], 64)
        minimum(second[0, 0][:, Q:H], acc[1, 0, Q][:], first[0, 0][:, 2:4, :], 64)
        minimum(second[0, H], acc[1, 0, H][:], first[0, H], 64)
        minimum(second[1, 0], acc[1, 1, 0][:, 0:H], first[1, 0], 64)
        quantise_w(2, 0, (0,))
        pieces(2, 0, ("acc200", "acc000", "acc00256"))

        POOL_SHARE = 32
        woven(2, 1, (0,))
        weave("gpsimd", 2, 1, 0, P - POOL_SHARE, P)
        weave("scalar", 2, 1, 0, 0, P - POOL_SHARE)
        quantise_w(2, 1, (0,))
        pieces(2, 1)
        second[1, H] = sbuf([P, H], F32, "second1h", at=0)[:]
        minimum(second[1, H], acc[1, 1, 0][:, H:S], first[1, H], 64)
        quantise_w(2, 0, (1,), place=4 * H)
        halves(2, 0, 1, ("acc010", "acc100"))
        w_bf[2, 1, 1] = (shared, 0)
        weave("gpsimd", 2, 1, 1, P - POOL_SHARE, P)
        weave("scalar", 2, 1, 1, 0, P - POOL_SHARE)
        quantise_w(2, 1, (1,))
        halves(2, 1, 1)

        last = raw[2, 1, 1][:].rearrange("p j n -> p (j n)")
        for m in range(2):
            for c0 in (0, H):
                result = last[:, c0 : c0 + H] if m == 0 else sbuf([P, H], F32, f"result{c0}")[:]
                if (m, c0) == (0, 0):
                    minimum(result[:, 0:Q], acc[2, 0, 0][:], second[0, 0][:, 0:Q])
                    minimum(result[:, Q:H], acc[2, 0, Q][:], second[0, 0][:, Q:H])
                else:
                    minimum(result, acc[2, m, c0][:], second[m, c0])
                nc.sync.dma_start(out=out[m * P : (m + 1) * P, c0 : c0 + H], in_=result)
